import numpy as np, ml_dtypes
CORES = [36,164,52,180,100,228,116,244]
N = 8
import mx_ref
BF = ml_dtypes.bfloat16
def entries(a):
    return np.ascontiguousarray(a.T).reshape(-1)
def table(e):
    return np.ascontiguousarray(np.reshape(e, (-1, 16)).T).astype(np.int32)
def cols(t, e):
    v = np.concatenate([t.reshape(128, -1, 4), np.zeros((128, 1, 4), BF)], axis=1)
    return np.ascontiguousarray(v[:, e]).reshape(128, -1)
def f(rng, *shape):
    return mx_ref.flush((rng.standard_normal(shape, dtype=np.float32) * np.exp2(rng.integers(-2, 3, shape[:-1] + (1,)))).astype(BF))
def wide(rng, *shape, cols=0):
    v = rng.standard_normal(shape, dtype=np.float32) * np.exp2(rng.integers(-12, 13, shape)).astype(np.float32)
    if cols: v *= np.repeat(np.exp2(rng.integers(-cols, cols + 1, shape[:-2] + (1, shape[-1] // 4))) * (rng.random(shape[:-2] + (1, shape[-1] // 4)) > 0.0625), 4, axis=-1).astype(np.float32)
    return mx_ref.flush(v.astype(BF))
T, CAPP = 256, 48
def lists(rng, full=False, skew=False, single=False, back=False):
    if full:
        v = rng.permutation(([CAPP] * (T // CAPP) + [T % CAPP] + [0] * N)[:N])
        n = v[(np.arange(N)[None, :] - np.arange(N)[:, None]) % N][rng.permutation(N)][:, rng.permutation(N)]
    else:
        n = np.full((N, N), T // N)
        for _ in range(20 * N):
            (s, t), (d, e) = rng.permutation(N)[:2], rng.permutation(N)[:2]
            k = rng.integers(0, min(n[s, d], n[t, e], CAPP - n[s, e], CAPP - n[t, d]) + 1)
            n[s, d] -= k; n[t, e] -= k; n[s, e] += k; n[t, d] += k
    a = np.full((N, N * CAPP), -1)
    for s in range(N):
        parts = np.split(rng.permutation(T), np.cumsum(n[s])[:-1])
        for d in range(N): a[s, d * CAPP + rng.permutation(CAPP)[:n[s, d]]] = parts[d]
    p, u, o = [], [], []
    for r in range(N):
        used = np.flatnonzero(a[:, r * CAPP:(r + 1) * CAPP].reshape(-1) >= 0)
        p.append(table(used[::-1] if back else rng.permutation(used)))
        h = rng.integers(0, N)
        c = rng.integers(0, 2, N) if full else (np.full(N, -1) if rng.random() < 0.5 else rng.integers(0, 2, N)) if single else rng.integers(-1, 2, N)
        if c[h] < 0: c[h] = rng.integers(0, 2)
        named = np.flatnonzero(c >= 0)
        if single: named = np.array([h])
        if skew:
            m = rng.integers(T // 2 + 1, T + 1)
            e = np.sort(np.concatenate([np.full(m, h), rng.choice(named, T - m)]))
        elif full: e = np.sort(np.concatenate([named, rng.choice(named, T - N)]))
        else: e = np.repeat(named, np.diff(np.concatenate([[0], np.sort(rng.integers(0, T + 1, len(named) - 1)), [T]])))
        u.append(table(np.concatenate([c, np.full(16 - N, -1)]))); o.append(table(e))
    return {"send": np.stack([table(k) for k in a]), "place": np.stack(p), "sel": np.stack(u), "of": np.stack(o)}
def setup_inputs(rng):
    return {"x": f(rng, N, 128, 4 * T), "w": f(rng, N, 256, 512), **lists(rng)}
def setup_inputs_full(rng):
    return {**setup_inputs(rng), **lists(rng, full=True)}
def setup_inputs_reversed(rng):
    return {**setup_inputs(rng), **lists(rng, back=True)}
def setup_inputs_single(rng):
    return {**setup_inputs(rng), **lists(rng, single=True)}
def setup_inputs_skew(rng):
    return {**setup_inputs(rng), **lists(rng, skew=True)}
def setup_inputs_spread(rng):
    d = setup_inputs(rng); d["x"] = wide(rng, N, 128, 4 * T, cols=8); return d
def check_inputs(d):
    b = []
    for k in ("x", "w"):
        a = np.abs(d[k].astype(np.float32))
        if not ((a == 0) | ((a >= 2.0 ** -30) & (a <= 2.0 ** 30))).all(): b.append(k)
    sends = np.stack([entries(d["send"][r]) for r in range(N)])
    for r in range(N):
        c, p, u, e = sends[r], entries(d["place"][r]), entries(d["sel"][r]), entries(d["of"][r])
        if c.min() < -1 or not np.array_equal(np.sort(c[c >= 0]), np.arange(T)): b.append("send")
        if not np.array_equal(np.sort(p), np.flatnonzero(sends[:, r * CAPP:(r + 1) * CAPP].reshape(-1) >= 0)): b.append("place")
        if u.min() < -1 or u.max() > 1 or (u[N:] != -1).any(): b.append("sel")
        if e.min() < 0 or e.max() >= N or (np.diff(e) < 0).any() or (u[e] < 0).any(): b.append("of")
    return b
def reference(x, w, send, place, sel, of):
    W = [[mx_ref.quantize(w[h][128 * m:128 * m + 128]) for m in range(2)] for h in range(N)]
    y = np.zeros((N, 128, T), np.float32)
    for r in range(N):
        slots = np.concatenate([cols(x[s], entries(send[s])[r * CAPP:(r + 1) * CAPP]) for s in range(N)], axis=1)
        X = mx_ref.quantize(cols(slots, entries(place[r])))
        u, e = entries(sel[r]), entries(of[r])
        for h in range(N):
            i = e == h
            if i.any(): y[r][:, i] = mx_ref.matmul(W[h][u[h]], X)[:, i]
    return {"y": y}

@@ -1,0 +1,354 @@
+from concourse.bass import DstId, RemoteDMATransfer
+from concourse.mybir import dt, AluOpType, ActivationFunctionType
+
+N, CAPP, TC = 8, 48, 256
+SLOTS = N * CAPP
+BOTH = (1,)
+PATH_E = {1: "D", 2: "D", 3: 1, 4: 2, 5: "D", 6: "D", 7: "D"}
+PATH_X = {1: 1, 2: 1, 3: 2, 4: 2, 5: 3, 6: "D", 7: "D"}
+GROUPS = ((2, 3), (4, 5), (6, 7))
+ORDER = (0, 1, 2, 5, 3, 6, 7, 4)
+VPART = 26
+NH = 3
+NE = N + len(BOTH)
+HALF = SLOTS // 2
+
+F8 = "float8_e4m3fn_x4"
+SCRATCH = {
+    "ldr": ("dram", [128, 1], "int32"), "lland": ("dram", [N, 128, 1], "int32"),
+    "snd": ("sbuf", [128, 24], "int32"), "off4": ("sbuf", [128, 24], "uint16"),
+    "pl": ("sbuf", [128, 16], "int32"), "ofl": ("sbuf", [128, 16], "int32"),
+    "selrow": ("sbuf", [1, 16], "int32"), "sf": ("sbuf", [1, 16], "float32"), "selb": ("sbuf", [128, 16], "float32"),
+    "lrow": ("sbuf", [1, 16], "int32"), "lf": ("sbuf", [1, 16], "float32"), "lb": ("sbuf", [128, 16], "float32"),
+    "ip": ("sbuf", [128, 32], "int32"), "iq": ("sbuf", [128, 32], "int32"), "ip15": ("sbuf", [128, 32], "int32"),
+    "ib": ("sbuf", [128, 32], "int32"), "offo": ("sbuf", [128, 32], "uint16"),
+    "offe": ("sbuf", [128, 64 * len(GROUPS)], "uint16"),
+    "ac0": ("sbuf", [128, 16], "float32"), "offy": ("sbuf", [128, 16], "uint16"), "sel3": ("sbuf", [128, 16], "float32"),
+    "xs": ("sbuf", [128, 4 * TC], "bfloat16"), "ws": ("sbuf", [128, 1024], "bfloat16"),
+    "xt": ("sbuf", [128, 4 * SLOTS], "bfloat16"), "eo": ("sbuf", [128, 512], "bfloat16"),
+    "xq": ("sbuf", [128, SLOTS], F8), "xqs": ("sbuf", [128, SLOTS], "uint8"),
+    "wq": ("sbuf", [128, 256], F8), "wqs": ("sbuf", [128, 256], "uint8"),
+    "xl": ("sbuf", [128, SLOTS], F8), "xls": ("sbuf", [128, SLOTS], "uint8"),
+    "el": ("sbuf", [128, 128 * NE], F8), "els": ("sbuf", [128, 128 * NE], "uint8"),
+    "ps": ("psum", [128, 4096], "float32"), "res": ("sbuf", [128, SLOTS * NE], "float32"), "yb": ("sbuf", [128, TC], "float32"),
+    "hx": ("sbuf", [128, 2 * CAPP], F8), "hxs": ("sbuf", [128, 2 * CAPP], "uint8"),
+    "he": ("sbuf", [128, 128], F8), "hes": ("sbuf", [128, 128], "uint8"),
+}
+for _i in range(len(BOTH)):
+    SCRATCH["ta%d" % _i] = ("sbuf", [128, 16], "float32")
+    SCRATCH["tb%d" % _i] = ("sbuf", [128, 16], "float32")
+    SCRATCH["aa%d" % _i] = ("sbuf", [128, 16], "float32")
+    SCRATCH["ab%d" % _i] = ("sbuf", [128, 16], "float32")
+SCRATCH["ac1"] = ("sbuf", [128, 16], "float32")
+for _i in range(len(GROUPS)):
+    SCRATCH["eg%d" % _i] = ("sbuf", [128, 512 * len(GROUPS[_i])], "bfloat16")
+    SCRATCH["gq%d" % _i] = ("sbuf", [128, 128 * len(GROUPS[_i])], F8)
+    SCRATCH["gs%d" % _i] = ("sbuf", [128, 128 * len(GROUPS[_i])], "uint8")
+
+SEMAPHORES = ["loc", "li", "xin", "hxc", "hxs", "hec", "hes", "ldr", "lown", "lsel", "lw", "lsnd", "lx", "lpl", "lrow", "xo", "y0", "y1",
+              "iot", "ib0", "ib", "sf", "selb", "offo", "qw", "off4", "xgv", "xgs", "qx", "og", "qo", "lf", "lb", "s3", "yv", "ys", "offy",
+              "evv", "evs"]
+SEMAPHORES += ["e%d" % k for k in range(1, N)] + ["ac%d" % k for k in range(2 + 4 * len(BOTH))]
+SEMAPHORES += ["%s%d" % (a, k) for a in ("go", "gv", "gs", "gq") for k in range(len(GROUPS))]
+SEMAPHORES += ["mm%d_%d" % (k, h) for k in range(NE) for h in range(2)] + ["ev%d_%d" % (k, h) for k in range(NE - 4) for h in range(2)]
+
+
+def share(engs, n):
+    w = 1
+    while 2 * w * n <= len(engs):
+        w *= 2
+    return [engs[i * w:(i + 1) * w] for i in range(n)]
+
+
+def bits(engs):
+    m = 0
+    for e in engs:
+        m |= 1 << e
+    return m
+
+
+def helpers_of(c, topo):
+    return [k for k in topo.cores_of(c) if topo.die(k) != topo.die(c)][:NH]
+
+
+def bases(r):
+    out, n = [], 0
+    for h in range(N):
+        out.append(n)
+        n += 2 if (r - h) % N in BOTH else 1
+    return out
+
+
+def u8(ap):
+    return ap.bitcast(dt.uint8)
+
+
+def rank_program(g, core, T, topo):
+    S = T.sem
+    rank = T.rank_of(core)
+    sent = [0]
+
+    def call(items):
+        tr = []
+        for cores, engs, src, dsts, sem in items:
+            ids = []
+            for c in cores:
+                rid, pid = topo.addr(c, core)
+                ids.append(DstId(rid=rid, pnc=pid))
+            tr.append(RemoteDMATransfer(dst_ids=ids, dma_engine_mask=bits(engs), remote_sem=sem, srcs=[src], dsts=dsts))
+            sent[0] += len(engs)
+        g.remote_dma_fused(tr, local_sem=S.loc)
+
+    if rank is None:
+        own = [c for c in topo.cores_of(core) if T.rank_of(c) is not None]
+        if not own or core not in helpers_of(own[0], topo):
+            return
+        r = T.rank_of(own[0])
+        me = helpers_of(own[0], topo).index(core) + 1
+        dest = lambda k: T.cores[(r + k) % N]
+        off = topo.engines(core, dest(1))
+        hi = [e for e in topo.engines(own[0], core) if e not in topo.engines(own[0], dest(1))]
+        xk = [k for k in range(1, N) if PATH_X[k] == me]
+        ek = [k for k in range(1, N) if PATH_E[k] == me]
+        if xk:
+            same = [h for h in range(1, NH + 1) if sum(PATH_X[k] == h for k in range(1, N)) == len(xk)]
+            n = len(share(hi, len(same))[0])
+            parts = share(off, len(xk))
+            g.wait_ge(S.hxc, n)
+            call([([dest(k)], parts[i], u8(T.hx[:, CAPP * i:CAPP * (i + 1)]), [u8(T.xl[:, CAPP * r:CAPP * (r + 1)])], S.xin) for i, k in enumerate(xk)])
+            g.wait_ge(S.hxs, n)
+            call([([dest(k)], parts[i], T.hxs[:, CAPP * i:CAPP * (i + 1)], [T.xls[:, CAPP * r:CAPP * (r + 1)]], S.xin) for i, k in enumerate(xk)])
+        for k in ek:
+            b = 128 * bases((r + k) % N)[r]
+            g.wait_ge(S.hec, len(hi))
+            call([([dest(k)], off, u8(T.he[:]), [u8(T.el[:, b:b + 128])], S["e%d" % k])])
+            g.wait_ge(S.hes, len(hi))
+            call([([dest(k)], off, T.hes[:], [T.els[:, b:b + 128]], S["e%d" % k])])
+        if sent[0]:
+            g.wait_ge(S.loc, sent[0])
+        return
+
+    r = rank
+    dest = lambda k: T.cores[(r + k) % N]
+    hlp = helpers_of(core, topo)
+    lo = topo.engines(core, dest(1))
+    hi = [e for e in topo.engines(core, hlp[0]) if e not in lo]
+    base = bases(r)
+    V, C, SY, TE = g.vector, g.scalar, g.sync, g.tensor
+    COPY = ActivationFunctionType.Copy
+    OP = AluOpType
+
+    SY.dma_start(T.ldr[0:16, :], T.sel[:, :]).then_inc(S.ldr, 16)
+    SY.dma_start(T.ldr[16:128, :], T.place[0:7, :]).then_inc(S.ldr, 16)
+    SY.dma_start(T.xs[:], T.x[:]).then_inc(S.lx, 16)
+    C.dma_start(T.ws[:, 0:512], T.w[0:128, :]).then_inc(S.lw, 16)
+    C.dma_start(T.ws[:, 512:1024], T.w[128:256, :]).then_inc(S.lw, 16)
+    for q in range(8):
+        (SY if q < 4 else C).dma_start(T.snd[16 * q:16 * q + 16, :], T.send[:, :]).then_inc(S.lsnd, 16)
+    SY.dma_start(T.selrow[0:1, :], T.sel[:, :]).then_inc(S.lsel, 16)
+    SY.dma_start(T.lland[r, 0:16, :], T.sel[:, :]).then_inc(S.lown, 16)
+
+    g.iota(T.ip[:], [[0, 32]], 0, 1).then_inc(S.iot, 1)
+    g.iota(T.iq[:], [[16, 32]], 0, 0).then_inc(S.iot, 1)
+    V.wait_ge(S.iot, 2)
+    V.tensor_scalar(T.ip15[:], T.ip[:], 15, None, OP.bitwise_and).then_inc(S.ib0, 1)
+    V.wait_ge(S.ib0, 1)
+    V.tensor_tensor(T.ib[:], T.ip15[:], T.iq[:], OP.add).then_inc(S.ib, 1)
+
+    g.wait_ge(S.ldr, 32)
+    call([([dest(k) for k in range(1, N)], lo[:1], T.ldr[:, :], [T.lland[r] for k in range(1, N)], S.li)])
+
+    V.wait_ge(S.lsel, 16)
+    V.tensor_scalar(T.sf[0:1, :], T.selrow[0:1, :], 0.0, 512.0, OP.max, OP.mult).then_inc(S.sf, 1)
+    g.wait_ge(S.sf, 1)
+    g.partition_broadcast(T.selb[:], T.sf[0:1, :], 128).then_inc(S.selb, 1)
+    V.wait_ge(S.lsnd, 128)
+    n = 1
+    V.tensor_scalar(T.off4[:, 0:3 * (N - r)], T.snd[:, 3 * r:24], 0.0, 4.0, OP.max, OP.mult).then_inc(S.off4, 1)
+    if r:
+        V.tensor_scalar(T.off4[:, 3 * (N - r):24], T.snd[:, 0:3 * r], 0.0, 4.0, OP.max, OP.mult).then_inc(S.off4, 1)
+        n = 2
+    V.wait_ge(S.lw, 32)
+    V.quantize_mx(T.wq[:], T.wqs[:], T.ws[:]).then_inc(S.qw, 1)
+
+    V.wait_ge(S.off4, n)
+    V.wait_ge(S.lx, 16)
+    for t in (0, 1):
+        V.tensor_copy(T.xt[:, t:4 * SLOTS:4], T.xs[:, t:4 * TC].indirect(T.off4[:, 0:24])).then_inc(S.xgv, 1)
+    C.wait_ge(S.off4, n)
+    C.wait_ge(S.lx, 16)
+    for t in (2, 3):
+        C.activation(T.xt[:, t:4 * SLOTS:4], T.xs[:, t:4 * TC].indirect(T.off4[:, 0:24]), COPY).then_inc(S.xgs, 1)
+    V.wait_ge(S.selb, 1)
+    V.wait_ge(S.ib, 1)
+    V.tensor_scalar(T.offo[:], T.ib[:], T.selb[:, r:r + 1], None, OP.add).then_inc(S.offo, 1)
+    V.wait_ge(S.xgv, 2)
+    V.wait_ge(S.xgs, 2)
+    V.quantize_mx(T.xq[:], T.xqs[:], T.xt[:]).then_inc(S.qx, 1)
+    C.wait_ge(S.offo, 1)
+    C.wait_ge(S.lw, 32)
+    C.activation(T.eo[:], T.ws[:].indirect(T.offo[:]), COPY).then_inc(S.og, 1)
+    V.wait_ge(S.og, 1)
+    b = 128 * base[r]
+    V.quantize_mx(T.el[:, b:b + 128], T.els[:, b:b + 128], T.eo[:]).then_inc(S.qo, 1)
+
+    g.wait_ge(S.qw, 1)
+    parts = share(lo, len(BOTH))
+    for sc in (0, 1):
+        it = []
+        for i, k in enumerate(BOTH):
+            b = 128 * bases((r + k) % N)[r]
+            src = T.wqs[:] if sc else u8(T.wq[:])
+            dst = T.els[:, b:b + 256] if sc else u8(T.el[:, b:b + 256])
+            it.append(([dest(k)], parts[i], src, [dst], S["e%d" % k]))
+        call(it)
+
+    sets = {}
+    for h in range(1, NH + 1):
+        ks = [k for k in range(1, N) if PATH_X[k] == h]
+        if ks:
+            sets.setdefault(len(ks), []).append((h, ks))
+    xd = [k for k in range(1, N) if PATH_X[k] == "D"]
+    if xd:
+        sets.setdefault(1, [])
+    g.wait_ge(S.qx, 1)
+    for sc in (0, 1):
+        for w in sorted(sets, reverse=True):
+            it = []
+            for i, (h, ks) in enumerate(sets[w]):
+                a = CAPP * ks[0]
+                src = T.xqs[:, a:a + CAPP * w] if sc else u8(T.xq[:, a:a + CAPP * w])
+                dst = T.hxs[:, 0:CAPP * w] if sc else u8(T.hx[:, 0:CAPP * w])
+                it.append(([hlp[h - 1]], share(hi, len(sets[w]))[i], src, [dst], S.hxs if sc else S.hxc))
+            if w == 1:
+                for i, k in enumerate(xd):
+                    src = T.xqs[:, CAPP * k:CAPP * (k + 1)] if sc else u8(T.xq[:, CAPP * k:CAPP * (k + 1)])
+                    dst = T.xls[:, CAPP * r:CAPP * (r + 1)] if sc else u8(T.xl[:, CAPP * r:CAPP * (r + 1)])
+                    it.append(([dest(k)], share(lo, len(xd))[i], src, [dst], S.xin))
+            call(it)
+    SY.wait_ge(S.qx, 1)
+    SY.dma_start(u8(T.xl[:, CAPP * r:CAPP * (r + 1)]), u8(T.xq[:, 0:CAPP])).then_inc(S.xo, 16)
+    SY.dma_start(T.xls[:, CAPP * r:CAPP * (r + 1)], T.xqs[:, 0:CAPP]).then_inc(S.xo, 16)
+
+    SY.wait_ge(S.lown, 16)
+    SY.wait_ge(S.li, N - 1)
+    SY.dma_start(T.lrow[0:1, :], T.lland[:, r:r + 2, 0]).then_inc(S.lrow, 16)
+    V.wait_ge(S.lrow, 16)
+    V.tensor_scalar(T.lf[0:1, :], T.lrow[0:1, :], 0.0, 512.0, OP.max, OP.mult).then_inc(S.lf, 1)
+    g.wait_ge(S.lf, 1)
+    g.partition_broadcast(T.lb[:], T.lf[0:1, :], 128).then_inc(S.lb, 1)
+    V.wait_ge(S.lb, 1)
+    for q in range(8):
+        SY.dma_start(T.pl[16 * q:16 * q + 16, :], T.place[:, :]).then_inc(S.lpl, 16)
+        SY.dma_start(T.ofl[16 * q:16 * q + 16, :], T.of[:, :]).then_inc(S.lpl, 16)
+
+    def offsets(j):
+        for i, k in enumerate(GROUPS[j]):
+            d = (r + k) % N
+            V.tensor_scalar(T.offe[:, 64 * j + 32 * i:64 * j + 32 * i + 32], T.ib[:], T.lb[:, 2 * d:2 * d + 1], None, OP.add).then_inc(S["go%d" % j], 1)
+
+    offsets(0)
+    for j, ks in enumerate(GROUPS):
+        eg, n = T["eg%d" % j], len(ks)
+        vp = VPART * n // 2
+        vp -= vp % 2
+        V.wait_ge(S["go%d" % j], n)
+        V.tensor_copy(eg[:, 0:16 * vp], T.ws[:].indirect(T.offe[:, 64 * j:64 * j + vp])).then_inc(S["gv%d" % j], 1)
+        C.wait_ge(S["go%d" % j], n)
+        C.activation(eg[:, 16 * vp:512 * n], T.ws[:].indirect(T.offe[:, 64 * j + vp:64 * j + 32 * n]), COPY).then_inc(S["gs%d" % j], 1)
+        if j + 1 < len(GROUPS):
+            offsets(j + 1)
+        V.wait_ge(S["gv%d" % j], 1)
+        V.wait_ge(S["gs%d" % j], 1)
+        V.quantize_mx(T["gq%d" % j][:], T["gs%d" % j][:], eg[:]).then_inc(S["gq%d" % j], 1)
+        g.wait_ge(S["gq%d" % j], 1)
+        ds = [k for k in ks if PATH_E[k] == "D"]
+        parts = share(lo, len(ds)) if ds else []
+        for sc in (0, 1):
+            it = []
+            for i, k in enumerate(ks):
+                src = T["gs%d" % j][:, 128 * i:128 * i + 128] if sc else u8(T["gq%d" % j][:, 128 * i:128 * i + 128])
+                if PATH_E[k] == "D":
+                    b = 128 * bases((r + k) % N)[r]
+                    dst = T.els[:, b:b + 128] if sc else u8(T.el[:, b:b + 128])
+                    it.append(([dest(k)], parts[ds.index(k)], src, [dst], S["e%d" % k]))
+                else:
+                    it.append(([hlp[PATH_E[k] - 1]], hi, src, [T.hes[:] if sc else u8(T.he[:])], S.hes if sc else S.hec))
+            call(it)
+
+    V.wait_ge(S.lpl, 256)
+    V.tensor_scalar(T.ac0[:], T.ofl[:], float(SLOTS), None, OP.mult).then_inc(S.ac0, 1)
+    V.tensor_scalar(T.sel3[:], T.selb[:], SLOTS / 512.0, None, OP.mult).then_inc(S.s3, 1)
+    V.wait_ge(S.ac0, 1)
+    V.tensor_tensor(T.ac1[:], T.ac0[:], T.pl[:], OP.add).then_inc(S.ac1, 1)
+    V.wait_ge(S.s3, 1)
+    acc, sn = T.ac1, 1
+    for i, k in enumerate(BOTH):
+        h = (r - k) % N
+        V.tensor_scalar(T["ta%d" % i][:], T.ofl[:], float(h), float(SLOTS), OP.is_gt, OP.mult).then_inc(S["ac%d" % (4 * i + 2)], 1)
+        V.tensor_scalar(T["tb%d" % i][:], T.ofl[:], float(h), T.sel3[:, h:h + 1], OP.is_equal, OP.mult).then_inc(S["ac%d" % (4 * i + 3)], 1)
+        V.wait_ge(S["ac%d" % sn], 1)
+        V.wait_ge(S["ac%d" % (4 * i + 2)], 1)
+        V.tensor_tensor(T["aa%d" % i][:], acc[:], T["ta%d" % i][:], OP.add).then_inc(S["ac%d" % (4 * i + 4)], 1)
+        V.wait_ge(S["ac%d" % (4 * i + 3)], 1)
+        V.wait_ge(S["ac%d" % (4 * i + 4)], 1)
+        V.tensor_tensor(T["ab%d" % i][:], T["aa%d" % i][:], T["tb%d" % i][:], OP.add).then_inc(S["ac%d" % (4 * i + 5)], 1)
+        acc, sn = T["ab%d" % i], 4 * i + 5
+    V.wait_ge(S["ac%d" % sn], 1)
+    V.tensor_copy(T.offy[:], acc[:]).then_inc(S.offy, 1)
+
+    def arrive_x(k):
+        if PATH_X[k] == "D":
+            return len(share(lo, len(xd))[0])
+        return len(share(lo, sum(PATH_X[q] == PATH_X[k] for q in range(1, N)))[0])
+
+    def arrive_e(k):
+        if k in BOTH:
+            return len(share(lo, len(BOTH))[0])
+        if PATH_E[k] != "D":
+            return len(lo)
+        gr = [ks for ks in GROUPS if k in ks][0]
+        return len(share(lo, sum(PATH_E[q] == "D" for q in gr))[0])
+
+    TE.wait_ge(S.xo, 32)
+    TE.wait_ge(S.xin, 2 * sum(arrive_x(k) for k in range(1, N)))
+    prods = []
+    for k in ORDER:
+        b = base[(r - k) % N]
+        prods.append((k, b, True))
+        if k in BOTH:
+            prods.append((k, b + 1, False))
+    for i, (k, b, first) in enumerate(prods):
+        if first:
+            TE.wait_ge(S["e%d" % k] if k else S.qo, 2 * arrive_e(k) if k else 1)
+        for h in (0, 1):
+            bank = (2 * i + h) % 8
+            if i >= 4:
+                TE.wait_ge(S["ev%d_%d" % (i - 4, h)], 1)
+            TE.matmul_mx(T.ps[:, 512 * bank:512 * bank + HALF], T.el[:, 128 * b:128 * b + 128], T.els[:, 128 * b:128 * b + 128],
+                         T.xl[:, HALF * h:HALF * (h + 1)], T.xls[:, HALF * h:HALF * (h + 1)], True, True).then_inc(S["mm%d_%d" % (i, h)], 1)
+            out = T.res[:, SLOTS * b + HALF * h:SLOTS * b + HALF * (h + 1)]
+            done = S["ev%d_%d" % (i, h)] if i < NE - 4 else (S.evs if h else S.evv)
+            if h == 0:
+                V.wait_ge(S["mm%d_0" % i], 1)
+                V.tensor_copy(out, T.ps[:, 512 * bank:512 * bank + HALF]).then_inc(done, 1)
+            else:
+                C.wait_ge(S["mm%d_1" % i], 1)
+                C.activation(out, T.ps[:, 512 * bank:512 * bank + HALF], COPY).then_inc(done, 1)
+
+    for q in (V, C):
+        q.wait_ge(S.offy, 1)
+        for i in range(NE - 4):
+            for h in (0, 1):
+                q.wait_ge(S["ev%d_%d" % (i, h)], 1)
+        q.wait_ge(S.evv, 4)
+        q.wait_ge(S.evs, 4)
+    V.tensor_copy(T.yb[:, 0:128], T.res[:].indirect(T.offy[:, 0:8])).then_inc(S.yv, 1)
+    C.activation(T.yb[:, 128:256], T.res[:].indirect(T.offy[:, 8:16]), COPY).then_inc(S.ys, 1)
+    SY.wait_ge(S.yv, 1)
+    SY.dma_start(T.y[:, 0:128], T.yb[:, 0:128]).then_inc(S.y0, 16)
+    C.wait_ge(S.ys, 1)
+    C.dma_start(T.y[:, 128:256], T.yb[:, 128:256]).then_inc(S.y1, 16)
+    SY.wait_ge(S.y0, 16)
+    C.wait_ge(S.y1, 16)
+    g.wait_ge(S.loc, sent[0])

@@ -3,17 +3,36 @@ from concourse.mybir import dt, AluOpType, ActivationFunctionType
 
 N, CAPP, TC = 8, 48, 256
 SLOTS = N * CAPP
-BOTH = (1,)
-PATH_E = {1: "D", 2: "D", 3: 1, 4: 2, 5: "D", 6: "D", 7: "D"}
-PATH_X = {1: 1, 2: 1, 3: 2, 4: 2, 5: 3, 6: "D", 7: "D"}
-GROUPS = ((2, 3), (4, 5), (6, 7))
-ORDER = (0, 1, 2, 5, 3, 6, 7, 4)
-VPART = 26
-NH = 3
-NE = N + len(BOTH)
-HALF = SLOTS // 2
+PAD = 128 - CAPP
+
+LO, HI, L0, L1 = (0, 8), (8, 8), (0, 4), (4, 4)
+EC, ES = ("Ec", 0, 1), ("Es", 0, 1)
+
+
+def pair(what, a, b):
+    return [((what, a, a), "D", a, L0), ((what, b, b), "D", b, L1)]
+
+
+def one(what, k):
+    return [((what, k, k), "D", k, LO)]
+
+
+PLAN = {
+    "chosen": (4, 5, 6, 7),
+    "xparts": ((1, 4), (5, 8)),
+    "mparts": ((0, 0), (1, 7)),
+    "rank": [[(("Xc", 1, 2), "H", 3, LO), (("Xc", 3, 4), "H", 5, HI)], [(("Xs", 1, 2), "H", 1, LO), (("Xs", 3, 4), "H", 6, HI)],
+             [(EC, "H", 0, HI)], pair("Xc", 5, 6), [(ES, "H", 2, HI)], one("Xc", 7), [(EC, "H", 4, HI)], pair("Xs", 5, 6), one("Xs", 7)]
+            + [one(w, k) for k in (4, 5, 6, 7) for w in ("Cc", "Cs")],
+    "help": {0: [[(EC, "D", k, LO)] for k in (1, 2)], 4: [[(EC, "D", 3, LO)]], 2: [[(ES, "D", k, LO)] for k in (1, 2, 3)],
+             1: [pair("Xs", 1, 2)], 6: [pair("Xs", 3, 4)], 3: [pair("Xc", 1, 2)], 5: [pair("Xc", 3, 4)]},
+    "order": [(k, 0, 7) for k in (0, 4, 5, 1, 6, 2, 3)] + [(7, 0, 7, "h")],
+    "wfirst": False,
+    "vpart": 14,
+}
 
 F8 = "float8_e4m3fn_x4"
+NE = 2 * N
 SCRATCH = {
     "ldr": ("dram", [128, 1], "int32"), "lland": ("dram", [N, 128, 1], "int32"),
     "snd": ("sbuf", [128, 24], "int32"), "off4": ("sbuf", [128, 24], "uint16"),
@@ -21,43 +40,27 @@ SCRATCH = {
     "selrow": ("sbuf", [1, 16], "int32"), "sf": ("sbuf", [1, 16], "float32"), "selb": ("sbuf", [128, 16], "float32"),
     "lrow": ("sbuf", [1, 16], "int32"), "lf": ("sbuf", [1, 16], "float32"), "lb": ("sbuf", [128, 16], "float32"),
     "ip": ("sbuf", [128, 32], "int32"), "iq": ("sbuf", [128, 32], "int32"), "ip15": ("sbuf", [128, 32], "int32"),
-    "ib": ("sbuf", [128, 32], "int32"), "offo": ("sbuf", [128, 32], "uint16"),
-    "offe": ("sbuf", [128, 64 * len(GROUPS)], "uint16"),
-    "ac0": ("sbuf", [128, 16], "float32"), "offy": ("sbuf", [128, 16], "uint16"), "sel3": ("sbuf", [128, 16], "float32"),
+    "ib": ("sbuf", [128, 32], "int32"), "offe": ("sbuf", [128, 32 * N], "uint16"),
+    "sel3": ("sbuf", [128, 16], "float32"), "tm": ("sbuf", [128, 16 * 16], "float32"), "t8": ("sbuf", [128, 128], "float32"),
+    "t4": ("sbuf", [128, 64], "float32"), "t2": ("sbuf", [128, 32], "float32"), "t1": ("sbuf", [128, 16], "float32"),
+    "offy": ("sbuf", [128, 16], "uint16"),
     "xs": ("sbuf", [128, 4 * TC], "bfloat16"), "ws": ("sbuf", [128, 1024], "bfloat16"),
-    "xt": ("sbuf", [128, 4 * SLOTS], "bfloat16"), "eo": ("sbuf", [128, 512], "bfloat16"),
+    "xt": ("sbuf", [128, 4 * SLOTS], "bfloat16"), "eg": ("sbuf", [128, 512 * N], "bfloat16"),
     "xq": ("sbuf", [128, SLOTS], F8), "xqs": ("sbuf", [128, SLOTS], "uint8"),
-    "wq": ("sbuf", [128, 256], F8), "wqs": ("sbuf", [128, 256], "uint8"),
-    "xl": ("sbuf", [128, SLOTS], F8), "xls": ("sbuf", [128, SLOTS], "uint8"),
+    "cq": ("sbuf", [128, 128 * N], F8), "cqs": ("sbuf", [128, 128 * N], "uint8"),
+    "xl": ("sbuf", [128, PAD + SLOTS], F8), "xls": ("sbuf", [128, PAD + SLOTS], "uint8"),
     "el": ("sbuf", [128, 128 * NE], F8), "els": ("sbuf", [128, 128 * NE], "uint8"),
     "ps": ("psum", [128, 4096], "float32"), "res": ("sbuf", [128, SLOTS * NE], "float32"), "yb": ("sbuf", [128, TC], "float32"),
-    "hx": ("sbuf", [128, 2 * CAPP], F8), "hxs": ("sbuf", [128, 2 * CAPP], "uint8"),
-    "he": ("sbuf", [128, 128], F8), "hes": ("sbuf", [128, 128], "uint8"),
+    "hx": ("sbuf", [128, SLOTS], F8), "hxs": ("sbuf", [128, SLOTS], "uint8"),
+    "he": ("sbuf", [128, 256], F8), "hes": ("sbuf", [128, 256], "uint8"),
+    "hc": ("sbuf", [128, 128 * N], F8), "hcs": ("sbuf", [128, 128 * N], "uint8"),
 }
-for _i in range(len(BOTH)):
-    SCRATCH["ta%d" % _i] = ("sbuf", [128, 16], "float32")
-    SCRATCH["tb%d" % _i] = ("sbuf", [128, 16], "float32")
-    SCRATCH["aa%d" % _i] = ("sbuf", [128, 16], "float32")
-    SCRATCH["ab%d" % _i] = ("sbuf", [128, 16], "float32")
-SCRATCH["ac1"] = ("sbuf", [128, 16], "float32")
-for _i in range(len(GROUPS)):
-    SCRATCH["eg%d" % _i] = ("sbuf", [128, 512 * len(GROUPS[_i])], "bfloat16")
-    SCRATCH["gq%d" % _i] = ("sbuf", [128, 128 * len(GROUPS[_i])], F8)
-    SCRATCH["gs%d" % _i] = ("sbuf", [128, 128 * len(GROUPS[_i])], "uint8")
-
-SEMAPHORES = ["loc", "li", "xin", "hxc", "hxs", "hec", "hes", "ldr", "lown", "lsel", "lw", "lsnd", "lx", "lpl", "lrow", "xo", "y0", "y1",
-              "iot", "ib0", "ib", "sf", "selb", "offo", "qw", "off4", "xgv", "xgs", "qx", "og", "qo", "lf", "lb", "s3", "yv", "ys", "offy",
-              "evv", "evs"]
-SEMAPHORES += ["e%d" % k for k in range(1, N)] + ["ac%d" % k for k in range(2 + 4 * len(BOTH))]
-SEMAPHORES += ["%s%d" % (a, k) for a in ("go", "gv", "gs", "gq") for k in range(len(GROUPS))]
-SEMAPHORES += ["mm%d_%d" % (k, h) for k in range(NE) for h in range(2)] + ["ev%d_%d" % (k, h) for k in range(NE - 4) for h in range(2)]
-
-
-def share(engs, n):
-    w = 1
-    while 2 * w * n <= len(engs):
-        w *= 2
-    return [engs[i * w:(i + 1) * w] for i in range(n)]
+NEV = 48
+SEMAPHORES = ["loc", "li", "ldr", "lsel", "lw", "lsnd", "lx", "lpl", "lrow", "y0", "iot", "ib0", "ib", "sf", "selb", "qw", "off4",
+              "qo", "lf", "lb", "s3", "yv", "ys", "offy", "mm", "evv", "evs", "tm", "t8", "t4", "t2", "t1"]
+SEMAPHORES += ["e%d" % k for k in range(1, N)] + ["xin%d" % k for k in range(4)] + ["h%d" % k for k in range(8)]
+SEMAPHORES += ["%s%d" % (a, k) for a in ("xgv", "xgs", "qx") for k in range(3)]
+SEMAPHORES += ["%s%d" % (a, k) for a in ("go", "gv", "gs", "gq", "li") for k in range(N)]
 
 
 def bits(engs):
@@ -68,15 +71,8 @@ def bits(engs):
 
 
 def helpers_of(c, topo):
-    return [k for k in topo.cores_of(c) if topo.die(k) != topo.die(c)][:NH]
-
-
-def bases(r):
-    out, n = [], 0
-    for h in range(N):
-        out.append(n)
-        n += 2 if (r - h) % N in BOTH else 1
-    return out
+    mine = [k for k in topo.cores_of(c) if k != c]
+    return [k for k in mine if topo.die(k) != topo.die(c)] + [k for k in mine if topo.die(k) == topo.die(c)]
 
 
 def u8(ap):
@@ -84,271 +80,306 @@ def u8(ap):
 
 
 def rank_program(g, core, T, topo):
-    S = T.sem
+    S, P = T.sem, PLAN
+    chosen = P["chosen"]
     rank = T.rank_of(core)
+    own = [c for c in topo.cores_of(core) if T.rank_of(c) is not None]
+    if not own:
+        return
+    r = T.rank_of(own[0])
+    hlp = helpers_of(own[0], topo)
+    dest = lambda k: T.cores[(r + k) % N]
+    lo = topo.engines(core, dest(1))
+    eng = lo + [e for e in topo.engines(core, [c for c in topo.cores_of(core) if c != core][0]) if e not in lo]
     sent = [0]
 
-    def call(items):
+    def view(piece, where, k=None):
+        what, a, b = piece
+        sc = what[1] == "s"
+        if what[0] == "X":
+            name, c0, n = {"src": "xq", "mid": "hx", "dst": "xl"}[where], CAPP * (a - 1), CAPP * (b - a + 1)
+            if where == "dst":
+                c0 = PAD + CAPP * (N - k)
+        elif what[0] == "E":
+            name, c0, n = {"src": "el", "mid": "he", "dst": "el"}[where], 128 * a, 128 * (b - a + 1)
+            if where != "mid":
+                c0 += 256 * r
+        else:
+            name, c0, n = {"src": "cq", "mid": "hc", "dst": "el"}[where], 128 * chosen.index(a), 128 * (b - a + 1)
+            if where == "dst":
+                c0 = 256 * r
+        return T[name + "s"][:, c0:c0 + n] if sc else u8(T[name][:, c0:c0 + n])
+
+    def xpart(k):
+        return [i for i, (a, b) in enumerate(P["mparts"]) if a <= N - k <= b][0]
+
+    def call(items, where):
         tr = []
-        for cores, engs, src, dsts, sem in items:
-            ids = []
-            for c in cores:
-                rid, pid = topo.addr(c, core)
-                ids.append(DstId(rid=rid, pnc=pid))
-            tr.append(RemoteDMATransfer(dst_ids=ids, dma_engine_mask=bits(engs), remote_sem=sem, srcs=[src], dsts=dsts))
-            sent[0] += len(engs)
+        for piece, kind, to, (e0, n) in items:
+            if kind == "D":
+                c, dv = dest(to), view(piece, "dst", to)
+                sem = S["xin%d" % xpart(to)] if piece[0][0] == "X" else S["e%d" % to]
+            else:
+                c, dv = hlp[to], view(piece, "mid")
+                sem = S["h%d" % inbox(to).index(piece)]
+            rid, pid = topo.addr(c, core)
+            tr.append(RemoteDMATransfer(dst_ids=[DstId(rid=rid, pnc=pid)], dma_engine_mask=bits(eng[e0:e0 + n]), remote_sem=sem,
+                                        srcs=[view(piece, where)], dsts=[dv]))
+            sent[0] += n
         g.remote_dma_fused(tr, local_sem=S.loc)
 
+    allcalls = list(P["rank"]) + [c for h in P["help"] for c in P["help"][h]]
+
+    def inbox(h):
+        return [p for items in allcalls for p, kind, to, e in items if kind == "H" and to == h]
+
+    def inbox_n(h, piece):
+        return [e[1] for items in allcalls for p, kind, to, e in items if kind == "H" and to == h and p == piece][0]
+
+    def arrive(test):
+        return sum(e[1] for items in allcalls for p, kind, to, e in items if kind == "D" and test(p, to))
+
     if rank is None:
-        own = [c for c in topo.cores_of(core) if T.rank_of(c) is not None]
-        if not own or core not in helpers_of(own[0], topo):
-            return
-        r = T.rank_of(own[0])
-        me = helpers_of(own[0], topo).index(core) + 1
-        dest = lambda k: T.cores[(r + k) % N]
-        off = topo.engines(core, dest(1))
-        hi = [e for e in topo.engines(own[0], core) if e not in topo.engines(own[0], dest(1))]
-        xk = [k for k in range(1, N) if PATH_X[k] == me]
-        ek = [k for k in range(1, N) if PATH_E[k] == me]
-        if xk:
-            same = [h for h in range(1, NH + 1) if sum(PATH_X[k] == h for k in range(1, N)) == len(xk)]
-            n = len(share(hi, len(same))[0])
-            parts = share(off, len(xk))
-            g.wait_ge(S.hxc, n)
-            call([([dest(k)], parts[i], u8(T.hx[:, CAPP * i:CAPP * (i + 1)]), [u8(T.xl[:, CAPP * r:CAPP * (r + 1)])], S.xin) for i, k in enumerate(xk)])
-            g.wait_ge(S.hxs, n)
-            call([([dest(k)], parts[i], T.hxs[:, CAPP * i:CAPP * (i + 1)], [T.xls[:, CAPP * r:CAPP * (r + 1)]], S.xin) for i, k in enumerate(xk)])
-        for k in ek:
-            b = 128 * bases((r + k) % N)[r]
-            g.wait_ge(S.hec, len(hi))
-            call([([dest(k)], off, u8(T.he[:]), [u8(T.el[:, b:b + 128])], S["e%d" % k])])
-            g.wait_ge(S.hes, len(hi))
-            call([([dest(k)], off, T.hes[:], [T.els[:, b:b + 128]], S["e%d" % k])])
+        me = hlp.index(core)
+        box, seen = inbox(me), []
+        for items in P["help"].get(me, []):
+            for p, kind, to, e in items:
+                for i, q in enumerate(box):
+                    if q[0] == p[0] and q[1] <= p[2] and p[1] <= q[2] and i not in seen:
+                        seen.append(i)
+                        g.wait_ge(S["h%d" % i], inbox_n(me, q))
+            call(items, "mid")
         if sent[0]:
             g.wait_ge(S.loc, sent[0])
         return
 
-    r = rank
-    dest = lambda k: T.cores[(r + k) % N]
-    hlp = helpers_of(core, topo)
-    lo = topo.engines(core, dest(1))
-    hi = [e for e in topo.engines(core, hlp[0]) if e not in lo]
-    base = bases(r)
     V, C, SY, TE = g.vector, g.scalar, g.sync, g.tensor
     COPY = ActivationFunctionType.Copy
     OP = AluOpType
 
-    SY.dma_start(T.ldr[0:16, :], T.sel[:, :]).then_inc(S.ldr, 16)
-    SY.dma_start(T.ldr[16:128, :], T.place[0:7, :]).then_inc(S.ldr, 16)
+    sb = P.get("sb")
+    if sb:
+        SY.dma_start(T.selrow[0:1, :], T.sel[:, :]).then_inc(S.lsel, 16)
+    elif chosen:
+        SY.dma_start(T.ldr[0:16, :], T.sel[:, :]).then_inc(S.ldr, 16)
+        C.dma_start(T.ldr[16:128, :], T.place[0:7, :]).then_inc(S.ldr, 16)
+
+    def load_w():
+        C.dma_start(T.ws[:, 0:512], T.w[0:128, :]).then_inc(S.lw, 16)
+        SY.dma_start(T.ws[:, 512:1024], T.w[128:256, :]).then_inc(S.lw, 16)
+
+    if P["wfirst"]:
+        load_w()
     SY.dma_start(T.xs[:], T.x[:]).then_inc(S.lx, 16)
-    C.dma_start(T.ws[:, 0:512], T.w[0:128, :]).then_inc(S.lw, 16)
-    C.dma_start(T.ws[:, 512:1024], T.w[128:256, :]).then_inc(S.lw, 16)
     for q in range(8):
-        (SY if q < 4 else C).dma_start(T.snd[16 * q:16 * q + 16, :], T.send[:, :]).then_inc(S.lsnd, 16)
-    SY.dma_start(T.selrow[0:1, :], T.sel[:, :]).then_inc(S.lsel, 16)
-    SY.dma_start(T.lland[r, 0:16, :], T.sel[:, :]).then_inc(S.lown, 16)
+        (SY if q < 3 else C).dma_start(T.snd[16 * q:16 * q + 16, :], T.send[:, :]).then_inc(S.lsnd, 16)
+    if not P["wfirst"]:
+        load_w()
+    if not sb:
+        SY.dma_start(T.selrow[0:1, :], T.sel[:, :]).then_inc(S.lsel, 16)
+    if not P.get("latepl"):
+        for q in range(8):
+            SY.dma_start(T.pl[16 * q:16 * q + 16, :], T.place[:, :]).then_inc(S.lpl, 16)
+            SY.dma_start(T.ofl[16 * q:16 * q + 16, :], T.of[:, :]).then_inc(S.lpl, 16)
 
-    g.iota(T.ip[:], [[0, 32]], 0, 1).then_inc(S.iot, 1)
-    g.iota(T.iq[:], [[16, 32]], 0, 0).then_inc(S.iot, 1)
-    V.wait_ge(S.iot, 2)
-    V.tensor_scalar(T.ip15[:], T.ip[:], 15, None, OP.bitwise_and).then_inc(S.ib0, 1)
-    V.wait_ge(S.ib0, 1)
-    V.tensor_tensor(T.ib[:], T.ip15[:], T.iq[:], OP.add).then_inc(S.ib, 1)
+    if chosen:
+        g.iota(T.ip[:], [[0, 32]], 0, 1).then_inc(S.iot, 1)
+        g.iota(T.iq[:], [[16, 32]], 0, 0).then_inc(S.iot, 1)
+        V.wait_ge(S.iot, 2)
+        V.tensor_scalar(T.ip15[:], T.ip[:], 15, None, OP.bitwise_and).then_inc(S.ib0, 1)
+        V.wait_ge(S.ib0, 1)
+        V.tensor_tensor(T.ib[:], T.ip15[:], T.iq[:], OP.add).then_inc(S.ib, 1)
+        ids = [topo.addr(dest(N - k), core) for k in chosen]
+    if sb:
+        V.wait_ge(S.lsel, 16)
+        V.tensor_scalar(T.sf[0:1, :], T.selrow[0:1, :], 0.0, 512.0, OP.max, OP.mult).then_inc(S.sf, 1)
+        g.wait_ge(S.sf, 1)
+        g.partition_broadcast(T.selb[:, 0:N], T.sf[0:1, 0:N], 128).then_inc(S.selb, 1)
+        g.wait_ge(S.selb, 1)
+        g.remote_dma_fused([RemoteDMATransfer(dst_ids=[DstId(rid=ids[i][0], pnc=ids[i][1])], dma_engine_mask=bits(lo[sb * i:sb * i + sb]), remote_sem=S["li%d" % k],
+                                              srcs=[T.selb[:, (r - k) % N:(r - k) % N + 1]], dsts=[T.lb[:, 2 * k:2 * k + 1]]) for i, k in enumerate(chosen)], local_sem=S.loc)
+        sent[0] += sb * len(chosen)
+    elif chosen:
+        g.wait_ge(S.ldr, 32)
+        g.remote_dma_fused([RemoteDMATransfer(dst_ids=[DstId(rid=a, pnc=b) for a, b in ids], dma_engine_mask=bits(lo[:1]), remote_sem=S.li,
+                                              srcs=[T.ldr[:, :]], dsts=[T.lland[k] for k in chosen])], local_sem=S.loc)
+        sent[0] += 1
 
-    g.wait_ge(S.ldr, 32)
-    call([([dest(k) for k in range(1, N)], lo[:1], T.ldr[:, :], [T.lland[r] for k in range(1, N)], S.li)])
+    def quant_w():
+        V.wait_ge(S.lw, 32)
+        V.quantize_mx(T.el[:, 256 * r:256 * r + 256], T.els[:, 256 * r:256 * r + 256], T.ws[:]).then_inc(S.qw, 1)
 
-    V.wait_ge(S.lsel, 16)
-    V.tensor_scalar(T.sf[0:1, :], T.selrow[0:1, :], 0.0, 512.0, OP.max, OP.mult).then_inc(S.sf, 1)
-    g.wait_ge(S.sf, 1)
-    g.partition_broadcast(T.selb[:], T.sf[0:1, :], 128).then_inc(S.selb, 1)
+    if P["wfirst"]:
+        quant_w()
     V.wait_ge(S.lsnd, 128)
-    n = 1
-    V.tensor_scalar(T.off4[:, 0:3 * (N - r)], T.snd[:, 3 * r:24], 0.0, 4.0, OP.max, OP.mult).then_inc(S.off4, 1)
-    if r:
-        V.tensor_scalar(T.off4[:, 3 * (N - r):24], T.snd[:, 0:3 * r], 0.0, 4.0, OP.max, OP.mult).then_inc(S.off4, 1)
-        n = 2
-    V.wait_ge(S.lw, 32)
-    V.quantize_mx(T.wq[:], T.wqs[:], T.ws[:]).then_inc(S.qw, 1)
+    a = 3 * ((r + 1) % N)
+    V.tensor_scalar(T.off4[:, 0:24 - a], T.snd[:, a:24], 0.0, 4.0, OP.max, OP.mult).then_inc(S.off4, 1)
+    if a:
+        V.tensor_scalar(T.off4[:, 24 - a:24], T.snd[:, 0:a], 0.0, 4.0, OP.max, OP.mult).then_inc(S.off4, 1)
+    for q in (V, C):
+        q.wait_ge(S.off4, 2 if a else 1)
+        q.wait_ge(S.lx, 16)
+    xp = P["xparts"]
 
-    V.wait_ge(S.off4, n)
-    V.wait_ge(S.lx, 16)
-    for t in (0, 1):
-        V.tensor_copy(T.xt[:, t:4 * SLOTS:4], T.xs[:, t:4 * TC].indirect(T.off4[:, 0:24])).then_inc(S.xgv, 1)
-    C.wait_ge(S.off4, n)
-    C.wait_ge(S.lx, 16)
-    for t in (2, 3):
-        C.activation(T.xt[:, t:4 * SLOTS:4], T.xs[:, t:4 * TC].indirect(T.off4[:, 0:24]), COPY).then_inc(S.xgs, 1)
-    V.wait_ge(S.selb, 1)
-    V.wait_ge(S.ib, 1)
-    V.tensor_scalar(T.offo[:], T.ib[:], T.selb[:, r:r + 1], None, OP.add).then_inc(S.offo, 1)
-    V.wait_ge(S.xgv, 2)
-    V.wait_ge(S.xgs, 2)
-    V.quantize_mx(T.xq[:], T.xqs[:], T.xt[:]).then_inc(S.qx, 1)
-    C.wait_ge(S.offo, 1)
-    C.wait_ge(S.lw, 32)
-    C.activation(T.eo[:], T.ws[:].indirect(T.offo[:]), COPY).then_inc(S.og, 1)
-    V.wait_ge(S.og, 1)
-    b = 128 * base[r]
-    V.quantize_mx(T.el[:, b:b + 128], T.els[:, b:b + 128], T.eo[:]).then_inc(S.qo, 1)
+    def xcols(i):
+        return CAPP * (xp[i][0] - 1), CAPP * xp[i][1]
 
-    g.wait_ge(S.qw, 1)
-    parts = share(lo, len(BOTH))
-    for sc in (0, 1):
-        it = []
-        for i, k in enumerate(BOTH):
-            b = 128 * bases((r + k) % N)[r]
-            src = T.wqs[:] if sc else u8(T.wq[:])
-            dst = T.els[:, b:b + 256] if sc else u8(T.el[:, b:b + 256])
-            it.append(([dest(k)], parts[i], src, [dst], S["e%d" % k]))
-        call(it)
+    def xquant(i):
+        c0, c1 = xcols(i)
+        V.wait_ge(S["xgv%d" % i], 2)
+        V.wait_ge(S["xgs%d" % i], 2)
+        V.quantize_mx(T.xq[:, c0:c1], T.xqs[:, c0:c1], T.xt[:, 4 * c0:4 * c1]).then_inc(S["qx%d" % i], 1)
 
-    sets = {}
-    for h in range(1, NH + 1):
-        ks = [k for k in range(1, N) if PATH_X[k] == h]
-        if ks:
-            sets.setdefault(len(ks), []).append((h, ks))
-    xd = [k for k in range(1, N) if PATH_X[k] == "D"]
-    if xd:
-        sets.setdefault(1, [])
-    g.wait_ge(S.qx, 1)
-    for sc in (0, 1):
-        for w in sorted(sets, reverse=True):
-            it = []
-            for i, (h, ks) in enumerate(sets[w]):
-                a = CAPP * ks[0]
-                src = T.xqs[:, a:a + CAPP * w] if sc else u8(T.xq[:, a:a + CAPP * w])
-                dst = T.hxs[:, 0:CAPP * w] if sc else u8(T.hx[:, 0:CAPP * w])
-                it.append(([hlp[h - 1]], share(hi, len(sets[w]))[i], src, [dst], S.hxs if sc else S.hxc))
-            if w == 1:
-                for i, k in enumerate(xd):
-                    src = T.xqs[:, CAPP * k:CAPP * (k + 1)] if sc else u8(T.xq[:, CAPP * k:CAPP * (k + 1)])
-                    dst = T.xls[:, CAPP * r:CAPP * (r + 1)] if sc else u8(T.xl[:, CAPP * r:CAPP * (r + 1)])
-                    it.append(([dest(k)], share(lo, len(xd))[i], src, [dst], S.xin))
-            call(it)
-    SY.wait_ge(S.qx, 1)
-    SY.dma_start(u8(T.xl[:, CAPP * r:CAPP * (r + 1)]), u8(T.xq[:, 0:CAPP])).then_inc(S.xo, 16)
-    SY.dma_start(T.xls[:, CAPP * r:CAPP * (r + 1)], T.xqs[:, 0:CAPP]).then_inc(S.xo, 16)
-
-    SY.wait_ge(S.lown, 16)
-    SY.wait_ge(S.li, N - 1)
-    SY.dma_start(T.lrow[0:1, :], T.lland[:, r:r + 2, 0]).then_inc(S.lrow, 16)
-    V.wait_ge(S.lrow, 16)
-    V.tensor_scalar(T.lf[0:1, :], T.lrow[0:1, :], 0.0, 512.0, OP.max, OP.mult).then_inc(S.lf, 1)
-    g.wait_ge(S.lf, 1)
-    g.partition_broadcast(T.lb[:], T.lf[0:1, :], 128).then_inc(S.lb, 1)
-    V.wait_ge(S.lb, 1)
-    for q in range(8):
-        SY.dma_start(T.pl[16 * q:16 * q + 16, :], T.place[:, :]).then_inc(S.lpl, 16)
-        SY.dma_start(T.ofl[16 * q:16 * q + 16, :], T.of[:, :]).then_inc(S.lpl, 16)
-
-    def offsets(j):
-        for i, k in enumerate(GROUPS[j]):
-            d = (r + k) % N
-            V.tensor_scalar(T.offe[:, 64 * j + 32 * i:64 * j + 32 * i + 32], T.ib[:], T.lb[:, 2 * d:2 * d + 1], None, OP.add).then_inc(S["go%d" % j], 1)
-
-    offsets(0)
-    for j, ks in enumerate(GROUPS):
-        eg, n = T["eg%d" % j], len(ks)
-        vp = VPART * n // 2
-        vp -= vp % 2
-        V.wait_ge(S["go%d" % j], n)
-        V.tensor_copy(eg[:, 0:16 * vp], T.ws[:].indirect(T.offe[:, 64 * j:64 * j + vp])).then_inc(S["gv%d" % j], 1)
-        C.wait_ge(S["go%d" % j], n)
-        C.activation(eg[:, 16 * vp:512 * n], T.ws[:].indirect(T.offe[:, 64 * j + vp:64 * j + 32 * n]), COPY).then_inc(S["gs%d" % j], 1)
-        if j + 1 < len(GROUPS):
-            offsets(j + 1)
-        V.wait_ge(S["gv%d" % j], 1)
-        V.wait_ge(S["gs%d" % j], 1)
-        V.quantize_mx(T["gq%d" % j][:], T["gs%d" % j][:], eg[:]).then_inc(S["gq%d" % j], 1)
-        g.wait_ge(S["gq%d" % j], 1)
-        ds = [k for k in ks if PATH_E[k] == "D"]
-        parts = share(lo, len(ds)) if ds else []
-        for sc in (0, 1):
-            it = []
-            for i, k in enumerate(ks):
-                src = T["gs%d" % j][:, 128 * i:128 * i + 128] if sc else u8(T["gq%d" % j][:, 128 * i:128 * i + 128])
-                if PATH_E[k] == "D":
-                    b = 128 * bases((r + k) % N)[r]
-                    dst = T.els[:, b:b + 128] if sc else u8(T.el[:, b:b + 128])
-                    it.append(([dest(k)], parts[ds.index(k)], src, [dst], S["e%d" % k]))
-                else:
-                    it.append(([hlp[PATH_E[k] - 1]], hi, src, [T.hes[:] if sc else u8(T.he[:])], S.hes if sc else S.hec))
-            call(it)
-
-    V.wait_ge(S.lpl, 256)
-    V.tensor_scalar(T.ac0[:], T.ofl[:], float(SLOTS), None, OP.mult).then_inc(S.ac0, 1)
-    V.tensor_scalar(T.sel3[:], T.selb[:], SLOTS / 512.0, None, OP.mult).then_inc(S.s3, 1)
-    V.wait_ge(S.ac0, 1)
-    V.tensor_tensor(T.ac1[:], T.ac0[:], T.pl[:], OP.add).then_inc(S.ac1, 1)
-    V.wait_ge(S.s3, 1)
-    acc, sn = T.ac1, 1
-    for i, k in enumerate(BOTH):
-        h = (r - k) % N
-        V.tensor_scalar(T["ta%d" % i][:], T.ofl[:], float(h), float(SLOTS), OP.is_gt, OP.mult).then_inc(S["ac%d" % (4 * i + 2)], 1)
-        V.tensor_scalar(T["tb%d" % i][:], T.ofl[:], float(h), T.sel3[:, h:h + 1], OP.is_equal, OP.mult).then_inc(S["ac%d" % (4 * i + 3)], 1)
-        V.wait_ge(S["ac%d" % sn], 1)
-        V.wait_ge(S["ac%d" % (4 * i + 2)], 1)
-        V.tensor_tensor(T["aa%d" % i][:], acc[:], T["ta%d" % i][:], OP.add).then_inc(S["ac%d" % (4 * i + 4)], 1)
-        V.wait_ge(S["ac%d" % (4 * i + 3)], 1)
-        V.wait_ge(S["ac%d" % (4 * i + 4)], 1)
-        V.tensor_tensor(T["ab%d" % i][:], T["aa%d" % i][:], T["tb%d" % i][:], OP.add).then_inc(S["ac%d" % (4 * i + 5)], 1)
-        acc, sn = T["ab%d" % i], 4 * i + 5
-    V.wait_ge(S["ac%d" % sn], 1)
-    V.tensor_copy(T.offy[:], acc[:]).then_inc(S.offy, 1)
-
-    def arrive_x(k):
-        if PATH_X[k] == "D":
-            return len(share(lo, len(xd))[0])
-        return len(share(lo, sum(PATH_X[q] == PATH_X[k] for q in range(1, N)))[0])
-
-    def arrive_e(k):
-        if k in BOTH:
-            return len(share(lo, len(BOTH))[0])
-        if PATH_E[k] != "D":
-            return len(lo)
-        gr = [ks for ks in GROUPS if k in ks][0]
-        return len(share(lo, sum(PATH_E[q] == "D" for q in gr))[0])
-
-    TE.wait_ge(S.xo, 32)
-    TE.wait_ge(S.xin, 2 * sum(arrive_x(k) for k in range(1, N)))
-    prods = []
-    for k in ORDER:
-        b = base[(r - k) % N]
-        prods.append((k, b, True))
-        if k in BOTH:
-            prods.append((k, b + 1, False))
-    for i, (k, b, first) in enumerate(prods):
-        if first:
-            TE.wait_ge(S["e%d" % k] if k else S.qo, 2 * arrive_e(k) if k else 1)
-        for h in (0, 1):
-            bank = (2 * i + h) % 8
-            if i >= 4:
-                TE.wait_ge(S["ev%d_%d" % (i - 4, h)], 1)
-            TE.matmul_mx(T.ps[:, 512 * bank:512 * bank + HALF], T.el[:, 128 * b:128 * b + 128], T.els[:, 128 * b:128 * b + 128],
-                         T.xl[:, HALF * h:HALF * (h + 1)], T.xls[:, HALF * h:HALF * (h + 1)], True, True).then_inc(S["mm%d_%d" % (i, h)], 1)
-            out = T.res[:, SLOTS * b + HALF * h:SLOTS * b + HALF * (h + 1)]
-            done = S["ev%d_%d" % (i, h)] if i < NE - 4 else (S.evs if h else S.evv)
-            if h == 0:
-                V.wait_ge(S["mm%d_0" % i], 1)
-                V.tensor_copy(out, T.ps[:, 512 * bank:512 * bank + HALF]).then_inc(done, 1)
+    for i in range(len(xp)):
+        c0, c1 = xcols(i)
+        for t in range(4):
+            src = T.xs[:, t:4 * TC].indirect(T.off4[:, c0 // 16:c1 // 16])
+            if t < 2:
+                V.tensor_copy(T.xt[:, 4 * c0 + t:4 * c1:4], src).then_inc(S["xgv%d" % i], 1)
             else:
-                C.wait_ge(S["mm%d_1" % i], 1)
-                C.activation(out, T.ps[:, 512 * bank:512 * bank + HALF], COPY).then_inc(done, 1)
+                C.activation(T.xt[:, 4 * c0 + t:4 * c1:4], src, COPY).then_inc(S["xgs%d" % i], 1)
+        xquant(i)
+        if i == 0 and not P["wfirst"]:
+            quant_w()
+    V.quantize_mx(T.xl[:, 0:128], T.xls[:, 0:128], T.xt[:, 4 * (SLOTS - 128):4 * SLOTS]).then_inc(S.qo, 1)
+
+    if not sb:
+        V.wait_ge(S.lsel, 16)
+        V.tensor_scalar(T.sf[0:1, :], T.selrow[0:1, :], 0.0, 512.0, OP.max, OP.mult).then_inc(S.sf, 1)
+
+    if chosen and not sb:
+        k0, k1 = min(chosen), max(chosen) + 1
+        SY.wait_ge(S.li, len(chosen))
+        SY.dma_start(T.lrow[0:1, 2 * k0:2 * k1], T.lland[k0:k1, r:r + 2, 0]).then_inc(S.lrow, 16)
+        V.wait_ge(S.lrow, 16)
+        V.tensor_scalar(T.lf[0:1, 2 * k0:2 * k1], T.lrow[0:1, 2 * k0:2 * k1], 0.0, 512.0, OP.max, OP.mult).then_inc(S.lf, 1)
+    if P.get("latepl"):
+        SY.wait_ge(S.qo, 1)
+        for q in range(8):
+            SY.dma_start(T.pl[16 * q:16 * q + 16, :], T.place[:, :]).then_inc(S.lpl, 16)
+            SY.dma_start(T.ofl[16 * q:16 * q + 16, :], T.of[:, :]).then_inc(S.lpl, 16)
+
+    waited = ["lb"] if sb else []
+    for items in P["rank"]:
+        if any(p[0][0] == "C" for p, _, _, _ in items) and "lb" not in waited:
+            waited.append("lb")
+            g.wait_ge(S.lf, 1)
+            g.partition_broadcast(T.lb[:, 2 * k0:2 * k1], T.lf[0:1, 2 * k0:2 * k1], 128).then_inc(S.lb, 1)
+            g.wait_ge(S.sf, 1)
+            g.partition_broadcast(T.selb[:, 0:N], T.sf[0:1, 0:N], 128).then_inc(S.selb, 1)
+        for p, _, _, _ in items:
+            if p[0][0] == "E":
+                need = ["qw"]
+            elif p[0][0] == "X":
+                need = ["qx%d" % i for i, (a, b) in enumerate(xp) if a <= p[2] and p[1] <= b]
+            else:
+                need = ["gq%d" % k for k in range(p[1], p[2] + 1)]
+            for s in need:
+                if s not in waited:
+                    waited.append(s)
+                    g.wait_ge(S[s], 1)
+        call(items, "src")
+    if "lb" not in waited:
+        g.wait_ge(S.sf, 1)
+        g.partition_broadcast(T.selb[:, 0:N], T.sf[0:1, 0:N], 128).then_inc(S.selb, 1)
+
+    if chosen:
+        if not sb:
+            V.wait_ge(S.lb, 1)
+        V.wait_ge(S.ib, 1)
+        vp = P["vpart"]
+        for i, k in enumerate(chosen):
+            if sb:
+                V.wait_ge(S["li%d" % k], sb)
+            V.tensor_scalar(T.offe[:, 32 * i:32 * i + 32], T.ib[:], T.lb[:, 2 * k:2 * k + 1], None, OP.add).then_inc(S["go%d" % k], 1)
+        for i, k in enumerate(chosen):
+            V.wait_ge(S["go%d" % k], 1)
+            V.tensor_copy(T.eg[:, 512 * i:512 * i + 16 * vp], T.ws[:].indirect(T.offe[:, 32 * i:32 * i + vp])).then_inc(S["gv%d" % k], 1)
+            C.wait_ge(S["go%d" % k], 1)
+            C.activation(T.eg[:, 512 * i + 16 * vp:512 * i + 512], T.ws[:].indirect(T.offe[:, 32 * i + vp:32 * i + 32]), COPY).then_inc(S["gs%d" % k], 1)
+            V.wait_ge(S["gv%d" % k], 1)
+            V.wait_ge(S["gs%d" % k], 1)
+            V.quantize_mx(T.cq[:, 128 * i:128 * i + 128], T.cqs[:, 128 * i:128 * i + 128], T.eg[:, 512 * i:512 * i + 512]).then_inc(S["gq%d" % k], 1)
+
+    both = [(r - k) % N for k in range(N) if k not in chosen]
+    base, n = [], 0
+    for h in range(N):
+        base.append(n)
+        n += 2 if h in both else 1
+    nres = n
+    V.wait_ge(S.lpl, 256)
+    V.wait_ge(S.selb, 1)
+    V.tensor_scalar(T.sel3[:, 0:N], T.selb[:, 0:N], SLOTS / 512.0, None, OP.mult).then_inc(S.s3, 1)
+    V.wait_ge(S.s3, 1)
+    terms = [(T.ofl, float(SLOTS), None, OP.mult, None), (T.pl, float(-CAPP * r), None, OP.add, None), (T.pl, float(CAPP * r), float(SLOTS), OP.is_lt, OP.mult)]
+    if chosen:
+        terms += [(T.ofl, float(h), float(SLOTS), OP.is_gt, OP.mult) for h in both if h < N - 1]
+    else:
+        terms[0] = (T.ofl, float(2 * SLOTS), None, OP.mult, None)
+    terms += [(T.ofl, float(h), T.sel3[:, h:h + 1], OP.is_equal, OP.mult) for h in both]
+    for i, (src, s1, s2, o1, o2) in enumerate(terms):
+        out = T.tm[:, 16 * i:16 * i + 16]
+        (V.tensor_scalar(out, src[:], s1, s2, o1, o2) if o2 else V.tensor_scalar(out, src[:], s1, None, o1)).then_inc(S.tm, 1)
+    n = len(terms)
+    if n < 16:
+        V.memset(T.tm[:, 16 * n:256], 0.0).then_inc(S.tm, 1)
+    V.wait_ge(S.tm, n + (n < 16))
+    src = T.tm
+    for name, w in (("t8", 128), ("t4", 64), ("t2", 32), ("t1", 16)):
+        V.tensor_tensor(T[name][:], src[:, 0:w], src[:, w:2 * w], OP.add).then_inc(S[name], 1)
+        V.wait_ge(S[name], 1)
+        src = T[name]
+    V.tensor_copy(T.offy[:], T.t1[:]).then_inc(S.offy, 1)
+
+    seen = []
+    nv = ns = nm = 0
+    who = []
+    for it in P["order"]:
+        k, ja, jb = it[:3]
+        h = (r - k) % N
+        need = [("qw", 1)] if k == 0 else [("e%d" % k, arrive(lambda p, to: p[0][0] != "X" and to == k))]
+        for i, (a, b) in enumerate(P["mparts"]):
+            if a <= jb and ja <= b:
+                if a == 0:
+                    need.append(("qo", 1))
+                if b > 0:
+                    need.append(("xin%d" % i, arrive(lambda p, to: p[0][0] == "X" and xpart(to) == i)))
+        for s, cnt in need:
+            if s not in seen:
+                seen.append(s)
+                TE.wait_ge(S[s], cnt)
+        c0, c1 = CAPP * ja, CAPP * (jb + 1)
+        skip = PAD if c1 - c0 < 128 else 0
+        for m in range(2 if h in both else 1):
+            e0 = 256 * h + 128 * m
+            cuts = [(c0, c1)] if len(it) == 3 else [(c0, (c0 + c1) // 2), ((c0 + c1) // 2, c1)]
+            for a, b in cuts:
+                bank = 512 * (nm % 8)
+                if nm >= 8:
+                    TE.wait_ge(*who[nm - 8])
+                TE.matmul_mx(T.ps[:, bank:bank + skip + b - a], T.el[:, e0:e0 + 128], T.els[:, e0:e0 + 128],
+                             T.xl[:, PAD + a - skip:PAD + b], T.xls[:, PAD + a - skip:PAD + b], True, True).then_inc(S.mm, 1)
+                nm += 1
+                out, src = T.res[:, SLOTS * (base[h] + m) + a:SLOTS * (base[h] + m) + b], T.ps[:, bank + skip:bank + skip + b - a]
+                if nm % 2:
+                    V.wait_ge(S.mm, nm)
+                    V.tensor_copy(out, src).then_inc(S.evv, 1)
+                    nv += 1
+                    who.append((S.evv, nv))
+                else:
+                    C.wait_ge(S.mm, nm)
+                    C.activation(out, src, COPY).then_inc(S.evs, 1)
+                    ns += 1
+                    who.append((S.evs, ns))
 
     for q in (V, C):
         q.wait_ge(S.offy, 1)
-        for i in range(NE - 4):
-            for h in (0, 1):
-                q.wait_ge(S["ev%d_%d" % (i, h)], 1)
-        q.wait_ge(S.evv, 4)
-        q.wait_ge(S.evs, 4)
-    V.tensor_copy(T.yb[:, 0:128], T.res[:].indirect(T.offy[:, 0:8])).then_inc(S.yv, 1)
-    C.activation(T.yb[:, 128:256], T.res[:].indirect(T.offy[:, 8:16]), COPY).then_inc(S.ys, 1)
+        q.wait_ge(S.evv, nv)
+        q.wait_ge(S.evs, ns)
+    V.tensor_copy(T.yb[:, 0:128], T.res[:, 0:SLOTS * nres].indirect(T.offy[:, 0:8])).then_inc(S.yv, 1)
+    C.activation(T.yb[:, 128:256], T.res[:, 0:SLOTS * nres].indirect(T.offy[:, 8:16]), COPY).then_inc(S.ys, 1)
     SY.wait_ge(S.yv, 1)
-    SY.dma_start(T.y[:, 0:128], T.yb[:, 0:128]).then_inc(S.y0, 16)
-    C.wait_ge(S.ys, 1)
-    C.dma_start(T.y[:, 128:256], T.yb[:, 128:256]).then_inc(S.y1, 16)
+    SY.wait_ge(S.ys, 1)
+    SY.dma_start(T.y[:, :], T.yb[:, :]).then_inc(S.y0, 16)
     SY.wait_ge(S.y0, 16)
-    C.wait_ge(S.y1, 16)
     g.wait_ge(S.loc, sent[0])

@@ -5,8 +5,8 @@ N, CAPP, TC = 8, 48, 256
 SLOTS = N * CAPP
 PAD = 128 - CAPP
 
-LO, HI, L0, L1 = (0, 8), (8, 8), (0, 4), (4, 4)
-EC, ES = ("Ec", 0, 1), ("Es", 0, 1)
+LO, HI, L0, L1, ALL = (0, 8), (8, 8), (0, 4), (4, 4), (0, 16)
+EC, ES, E0, E1 = ("Ec", 0, 1), ("Es", 0, 1), ("Ec", 0, 0), ("Ec", 1, 1)
 
 
 def pair(what, a, b):
@@ -19,16 +19,36 @@ def one(what, k):
 
 PLAN = {
     "chosen": (4, 5, 6, 7),
-    "xparts": ((1, 4), (5, 8)),
-    "mparts": ((0, 0), (1, 7)),
-    "rank": [[(("Xc", 1, 2), "H", 3, LO), (("Xc", 3, 4), "H", 5, HI)], [(("Xs", 1, 2), "H", 1, LO), (("Xs", 3, 4), "H", 6, HI)],
-             [(EC, "H", 0, HI)], pair("Xc", 5, 6), [(ES, "H", 2, HI)], one("Xc", 7), [(EC, "H", 4, HI)], pair("Xs", 5, 6), one("Xs", 7)]
-            + [one(w, k) for k in (4, 5, 6, 7) for w in ("Cc", "Cs")],
-    "help": {0: [[(EC, "D", k, LO)] for k in (1, 2)], 4: [[(EC, "D", 3, LO)]], 2: [[(ES, "D", k, LO)] for k in (1, 2, 3)],
-             1: [pair("Xs", 1, 2)], 6: [pair("Xs", 3, 4)], 3: [pair("Xc", 1, 2)], 5: [pair("Xc", 3, 4)]},
-    "order": [(k, 0, 7) for k in (0, 4, 5, 1, 6, 2, 3)] + [(7, 0, 7, "h")],
+    "xparts": ((0, 192), (192, 384)),
+    "xv": (2, 1),
+    "mparts": ((0, 3), (4, 7)),
+    "rank": [[(("Xs", 1, 2), "H", 6, LO), (("Xs", 3, 4), "H", 5, HI)], [(("Xc", 3, 3), "H", 1, LO), (("Xc", 4, 4), "H", 0, HI)],
+             pair("Xc", 1, 2), [(EC, "H", 1, HI)], [(("Xs", 5, 7), "H", 6, HI)], pair("Xc", 5, 6), one("Xc", 7),
+             [(EC, "D", 3, LO)], [(ES, "H", 5, HI), (ES, "D", 3, LO)],
+             [(("Cc", 4, 4), "H", 0, HI)], [(("Cs", 4, 4), "H", 0, HI)]]
+            + [one(w, k) for k in (5, 6, 7) for w in ("Cc", "Cs")],
+    "help": {0: [one("Xc", 4), one("Cc", 4), one("Cs", 4)],
+             1: [one("Xc", 3), [(EC, "D", 1, LO)], [(EC, "D", 2, LO)]],
+             5: [one("Xs", 3), one("Xs", 4), [(ES, "D", 1, LO)], [(ES, "D", 2, LO)]],
+             6: [one("Xs", k) for k in (1, 2, 5, 6, 7)]},
+    "order": [(0, 4, 7), (3, 4, 7), (0, 0, 3), (3, 0, 3), (1, 0, 7), (5, 0, 7, "h"), (6, 0, 7, "h"), (2, 0, 7), (4, 0, 7, "h"), (7, 0, 7, "h")],
     "wfirst": False,
-    "vpart": 14,
+    "vpart": 12,
+    "vfirst": 16,
+    "ownc": True,
+    "le": 2,
+    "fill": True,
+    "sy": 1,
+    "early": 0,
+    "selat": 0,
+    "sb": (),
+    "ahead": True,
+    "groups": 2,
+    "qwat": 1,
+    "fillers": (2, 3),
+    "sfirst": 1,
+    "lfat": 0,
+    "lbat": 0,
 }
 
 F8 = "float8_e4m3fn_x4"
@@ -39,14 +59,16 @@ SCRATCH = {
     "pl": ("sbuf", [128, 16], "int32"), "ofl": ("sbuf", [128, 16], "int32"),
     "selrow": ("sbuf", [1, 16], "int32"), "sf": ("sbuf", [1, 16], "float32"), "selb": ("sbuf", [128, 16], "float32"),
     "lrow": ("sbuf", [1, 16], "int32"), "lf": ("sbuf", [1, 16], "float32"), "lb": ("sbuf", [128, 16], "float32"),
+    "lbs": ("sbuf", [128, N], "float32"),
     "ip": ("sbuf", [128, 32], "int32"), "iq": ("sbuf", [128, 32], "int32"), "ip15": ("sbuf", [128, 32], "int32"),
-    "ib": ("sbuf", [128, 32], "int32"), "offe": ("sbuf", [128, 32 * N], "uint16"),
-    "sel3": ("sbuf", [128, 16], "float32"), "tm": ("sbuf", [128, 16 * 16], "float32"), "t8": ("sbuf", [128, 128], "float32"),
+    "ib": ("sbuf", [128, 32], "int32"), "offe": ("sbuf", [128, 32 * N], "uint16"), "offo": ("sbuf", [128, 32], "uint16"),
+    "sel3": ("sbuf", [128, 16], "float32"), "tm": ("sbuf", [128, 16 * 8], "float32"),
     "t4": ("sbuf", [128, 64], "float32"), "t2": ("sbuf", [128, 32], "float32"), "t1": ("sbuf", [128, 16], "float32"),
     "offy": ("sbuf", [128, 16], "uint16"),
     "xs": ("sbuf", [128, 4 * TC], "bfloat16"), "ws": ("sbuf", [128, 1024], "bfloat16"),
-    "xt": ("sbuf", [128, 4 * SLOTS], "bfloat16"), "eg": ("sbuf", [128, 512 * N], "bfloat16"),
+    "xt": ("sbuf", [128, 4 * SLOTS], "bfloat16"), "eg": ("sbuf", [128, 512 * N], "bfloat16"), "eo": ("sbuf", [128, 512], "bfloat16"),
     "xq": ("sbuf", [128, SLOTS], F8), "xqs": ("sbuf", [128, SLOTS], "uint8"),
+    "wq": ("sbuf", [128, 256], F8), "wqs": ("sbuf", [128, 256], "uint8"),
     "cq": ("sbuf", [128, 128 * N], F8), "cqs": ("sbuf", [128, 128 * N], "uint8"),
     "xl": ("sbuf", [128, PAD + SLOTS], F8), "xls": ("sbuf", [128, PAD + SLOTS], "uint8"),
     "el": ("sbuf", [128, 128 * NE], F8), "els": ("sbuf", [128, 128 * NE], "uint8"),
@@ -55,12 +77,11 @@ SCRATCH = {
     "he": ("sbuf", [128, 256], F8), "hes": ("sbuf", [128, 256], "uint8"),
     "hc": ("sbuf", [128, 128 * N], F8), "hcs": ("sbuf", [128, 128 * N], "uint8"),
 }
-NEV = 48
-SEMAPHORES = ["loc", "li", "ldr", "lsel", "lw", "lsnd", "lx", "lpl", "lrow", "y0", "iot", "ib0", "ib", "sf", "selb", "qw", "off4",
-              "qo", "lf", "lb", "s3", "yv", "ys", "offy", "mm", "evv", "evs", "tm", "t8", "t4", "t2", "t1"]
+SEMAPHORES = ["loc", "li", "ldr", "lsel", "lw", "lsnd", "lx", "lpl", "lrow", "y0", "iot", "ib0", "ib", "sf", "selb", "qw", "off4", "oo", "og", "qe",
+              "qo", "lf", "lb", "s3", "yv", "ys", "offy", "mm", "evv", "evs", "tm", "t4", "t2", "t1"]
 SEMAPHORES += ["e%d" % k for k in range(1, N)] + ["xin%d" % k for k in range(4)] + ["h%d" % k for k in range(8)]
 SEMAPHORES += ["%s%d" % (a, k) for a in ("xgv", "xgs", "qx") for k in range(3)]
-SEMAPHORES += ["%s%d" % (a, k) for a in ("go", "gv", "gs", "gq", "li") for k in range(N)]
+SEMAPHORES += ["%s%d" % (a, k) for a in ("go", "gv", "gs", "gq", "ls") for k in range(N)]
 
 
 def bits(engs):
@@ -101,8 +122,8 @@ def rank_program(g, core, T, topo):
             if where == "dst":
                 c0 = PAD + CAPP * (N - k)
         elif what[0] == "E":
-            name, c0, n = {"src": "el", "mid": "he", "dst": "el"}[where], 128 * a, 128 * (b - a + 1)
-            if where != "mid":
+            name, c0, n = {"src": "wq", "mid": "he", "dst": "el"}[where], 128 * a, 128 * (b - a + 1)
+            if where == "dst":
                 c0 += 256 * r
         else:
             name, c0, n = {"src": "cq", "mid": "hc", "dst": "el"}[where], 128 * chosen.index(a), 128 * (b - a + 1)
@@ -156,122 +177,151 @@ def rank_program(g, core, T, topo):
     V, C, SY, TE = g.vector, g.scalar, g.sync, g.tensor
     COPY = ActivationFunctionType.Copy
     OP = AluOpType
+    ownc = P["ownc"]
 
-    sb = P.get("sb")
+    sb = P["sb"]
+    ng = P["groups"]
+    pn = 16 * ng
+
+    def spread(buf, sem, n):
+        have = pn
+        while have < 128:
+            V.wait_ge(sem, n)
+            V.tensor_copy(buf[have:2 * have, :], buf[0:have, :]).then_inc(sem, 1)
+            have, n = 2 * have, n + 1
+        return n
+
+    far = chosen[len(sb):]
     if sb:
         SY.dma_start(T.selrow[0:1, :], T.sel[:, :]).then_inc(S.lsel, 16)
-    elif chosen:
-        SY.dma_start(T.ldr[0:16, :], T.sel[:, :]).then_inc(S.ldr, 16)
+    if far:
+        (C if sb else SY).dma_start(T.ldr[0:16, :], T.sel[:, :]).then_inc(S.ldr, 16)
         C.dma_start(T.ldr[16:128, :], T.place[0:7, :]).then_inc(S.ldr, 16)
 
     def load_w():
-        C.dma_start(T.ws[:, 0:512], T.w[0:128, :]).then_inc(S.lw, 16)
+        (SY if ng < 8 else C).dma_start(T.ws[:, 0:512], T.w[0:128, :]).then_inc(S.lw, 16)
         SY.dma_start(T.ws[:, 512:1024], T.w[128:256, :]).then_inc(S.lw, 16)
+
+    def load_send(qs, queue):
+        for q in qs:
+            queue.dma_start(T.snd[16 * q:16 * q + 16, :], T.send[:, :]).then_inc(S.lsnd, 16)
 
     if P["wfirst"]:
         load_w()
+    load_send(range(P["sy"]), SY)
     SY.dma_start(T.xs[:], T.x[:]).then_inc(S.lx, 16)
-    for q in range(8):
-        (SY if q < 3 else C).dma_start(T.snd[16 * q:16 * q + 16, :], T.send[:, :]).then_inc(S.lsnd, 16)
+    load_send(range(P["sy"], ng), C)
+    if not sb:
+        (C if ng < 8 else SY).dma_start(T.selrow[0:1, :], T.sel[:, :]).then_inc(S.lsel, 16)
     if not P["wfirst"]:
         load_w()
-    if not sb:
-        SY.dma_start(T.selrow[0:1, :], T.sel[:, :]).then_inc(S.lsel, 16)
-    if not P.get("latepl"):
-        for q in range(8):
-            SY.dma_start(T.pl[16 * q:16 * q + 16, :], T.place[:, :]).then_inc(S.lpl, 16)
-            SY.dma_start(T.ofl[16 * q:16 * q + 16, :], T.of[:, :]).then_inc(S.lpl, 16)
+    for q in range(ng):
+        SY.dma_start(T.pl[16 * q:16 * q + 16, :], T.place[:, :]).then_inc(S.lpl, 16)
+        SY.dma_start(T.ofl[16 * q:16 * q + 16, :], T.of[:, :]).then_inc(S.lpl, 16)
 
-    if chosen:
-        g.iota(T.ip[:], [[0, 32]], 0, 1).then_inc(S.iot, 1)
-        g.iota(T.iq[:], [[16, 32]], 0, 0).then_inc(S.iot, 1)
-        V.wait_ge(S.iot, 2)
-        V.tensor_scalar(T.ip15[:], T.ip[:], 15, None, OP.bitwise_and).then_inc(S.ib0, 1)
-        V.wait_ge(S.ib0, 1)
-        V.tensor_tensor(T.ib[:], T.ip15[:], T.iq[:], OP.add).then_inc(S.ib, 1)
-        ids = [topo.addr(dest(N - k), core) for k in chosen]
-    if sb:
+    g.iota(T.ip[:], [[0, 32]], 0, 1).then_inc(S.iot, 1)
+    g.iota(T.iq[:], [[16, 32]], 0, 0).then_inc(S.iot, 1)
+    V.wait_ge(S.iot, 2)
+    V.tensor_scalar(T.ip15[:], T.ip[:], 15, None, OP.bitwise_and).then_inc(S.ib0, 1)
+    V.wait_ge(S.ib0, 1)
+    V.tensor_tensor(T.ib[:], T.ip15[:], T.iq[:], OP.add).then_inc(S.ib, 1)
+
+    def sel_row():
         V.wait_ge(S.lsel, 16)
         V.tensor_scalar(T.sf[0:1, :], T.selrow[0:1, :], 0.0, 512.0, OP.max, OP.mult).then_inc(S.sf, 1)
+
+    def sel_all():
         g.wait_ge(S.sf, 1)
         g.partition_broadcast(T.selb[:, 0:N], T.sf[0:1, 0:N], 128).then_inc(S.selb, 1)
+
+    tr, used = [], 0
+    ident = lambda k: [DstId(rid=topo.addr(dest(N - k), core)[0], pnc=topo.addr(dest(N - k), core)[1])]
+    if sb:
+        sel_row()
+        sel_all()
         g.wait_ge(S.selb, 1)
-        g.remote_dma_fused([RemoteDMATransfer(dst_ids=[DstId(rid=ids[i][0], pnc=ids[i][1])], dma_engine_mask=bits(lo[sb * i:sb * i + sb]), remote_sem=S["li%d" % k],
-                                              srcs=[T.selb[:, (r - k) % N:(r - k) % N + 1]], dsts=[T.lb[:, 2 * k:2 * k + 1]]) for i, k in enumerate(chosen)], local_sem=S.loc)
-        sent[0] += sb * len(chosen)
-    elif chosen:
+        for k, n in zip(chosen, sb):
+            h = (r - k) % N
+            tr.append(RemoteDMATransfer(dst_ids=ident(k), dma_engine_mask=bits(lo[used:used + n]), remote_sem=S["ls%d" % k],
+                                        srcs=[T.selb[:, h:h + 1]], dsts=[T.lbs[:, k:k + 1]]))
+            used += n
+    nle = 0
+    if far:
         g.wait_ge(S.ldr, 32)
-        g.remote_dma_fused([RemoteDMATransfer(dst_ids=[DstId(rid=a, pnc=b) for a, b in ids], dma_engine_mask=bits(lo[:1]), remote_sem=S.li,
-                                              srcs=[T.ldr[:, :]], dsts=[T.lland[k] for k in chosen])], local_sem=S.loc)
-        sent[0] += 1
+        rest = lo[used:]
+        two = min(len(far), len(rest) - len(far)) if P["le"] == 2 else 0
+        le = [rest[2 * i:2 * i + 2] if i < two else rest[two + i:two + i + 1] for i in range(len(far))]
+        nle = sum(len(e) for e in le)
+        tr += [RemoteDMATransfer(dst_ids=ident(k), dma_engine_mask=bits(le[i]), remote_sem=S.li, srcs=[T.ldr[:, :]], dsts=[T.lland[k]])
+               for i, k in enumerate(far)]
+    g.remote_dma_fused(tr, local_sem=S.loc)
+    sent[0] += nle + used
 
     def quant_w():
         V.wait_ge(S.lw, 32)
-        V.quantize_mx(T.el[:, 256 * r:256 * r + 256], T.els[:, 256 * r:256 * r + 256], T.ws[:]).then_inc(S.qw, 1)
+        V.quantize_mx(T.wq[:], T.wqs[:], T.ws[:]).then_inc(S.qw, 1)
 
     if P["wfirst"]:
         quant_w()
-    V.wait_ge(S.lsnd, 128)
+    V.wait_ge(S.lsnd, 16 * ng)
     a = 3 * ((r + 1) % N)
-    V.tensor_scalar(T.off4[:, 0:24 - a], T.snd[:, a:24], 0.0, 4.0, OP.max, OP.mult).then_inc(S.off4, 1)
+    V.tensor_scalar(T.off4[0:pn, 0:24 - a], T.snd[0:pn, a:24], 0.0, 4.0, OP.max, OP.mult).then_inc(S.off4, 1)
     if a:
-        V.tensor_scalar(T.off4[:, 24 - a:24], T.snd[:, 0:a], 0.0, 4.0, OP.max, OP.mult).then_inc(S.off4, 1)
+        V.tensor_scalar(T.off4[0:pn, 24 - a:24], T.snd[0:pn, 0:a], 0.0, 4.0, OP.max, OP.mult).then_inc(S.off4, 1)
+    noff = spread(T.off4, S.off4, 2 if a else 1)
+    if not sb and P["selat"] >= 0:
+        sel_row()
     for q in (V, C):
-        q.wait_ge(S.off4, 2 if a else 1)
+        q.wait_ge(S.off4, noff)
         q.wait_ge(S.lx, 16)
     xp = P["xparts"]
-
-    def xcols(i):
-        return CAPP * (xp[i][0] - 1), CAPP * xp[i][1]
-
-    def xquant(i):
-        c0, c1 = xcols(i)
-        V.wait_ge(S["xgv%d" % i], 2)
-        V.wait_ge(S["xgs%d" % i], 2)
-        V.quantize_mx(T.xq[:, c0:c1], T.xqs[:, c0:c1], T.xt[:, 4 * c0:4 * c1]).then_inc(S["qx%d" % i], 1)
-
     for i in range(len(xp)):
-        c0, c1 = xcols(i)
+        c0, c1, nv = xp[i][0], xp[i][1], P["xv"][i]
         for t in range(4):
             src = T.xs[:, t:4 * TC].indirect(T.off4[:, c0 // 16:c1 // 16])
-            if t < 2:
+            if t < nv:
                 V.tensor_copy(T.xt[:, 4 * c0 + t:4 * c1:4], src).then_inc(S["xgv%d" % i], 1)
             else:
                 C.activation(T.xt[:, 4 * c0 + t:4 * c1:4], src, COPY).then_inc(S["xgs%d" % i], 1)
-        xquant(i)
-        if i == 0 and not P["wfirst"]:
+        if i == P["qwat"] and not P["wfirst"]:
             quant_w()
-    V.quantize_mx(T.xl[:, 0:128], T.xls[:, 0:128], T.xt[:, 4 * (SLOTS - 128):4 * SLOTS]).then_inc(S.qo, 1)
+        V.wait_ge(S["xgv%d" % i], nv)
+        V.wait_ge(S["xgs%d" % i], 4 - nv)
+        V.quantize_mx(T.xq[:, c0:c1], T.xqs[:, c0:c1], T.xt[:, 4 * c0:4 * c1]).then_inc(S["qx%d" % i], 1)
 
-    if not sb:
-        V.wait_ge(S.lsel, 16)
-        V.tensor_scalar(T.sf[0:1, :], T.selrow[0:1, :], 0.0, 512.0, OP.max, OP.mult).then_inc(S.sf, 1)
+    V.wait_ge(S.ib, 1)
+    if ownc:
+        V.wait_ge(S.selb, 1)
+        V.tensor_scalar(T.offo[:], T.ib[:], T.selb[:, r:r + 1], None, OP.add).then_inc(S.oo, 1)
+        C.wait_ge(S.oo, 1)
+        C.wait_ge(S.lw, 32)
+        C.activation(T.eo[:], T.ws[:].indirect(T.offo[:]), COPY).then_inc(S.og, 1)
 
-    if chosen and not sb:
-        k0, k1 = min(chosen), max(chosen) + 1
-        SY.wait_ge(S.li, len(chosen))
+    def own_slots():
+        V.quantize_mx(T.xl[:, 0:128], T.xls[:, 0:128], T.xt[:, 4 * (SLOTS - 128):4 * SLOTS]).then_inc(S.qo, 1)
+
+    own_slots()
+
+    if far:
+        k0, k1 = min(far), max(far) + 1
+        SY.wait_ge(S.li, nle)
         SY.dma_start(T.lrow[0:1, 2 * k0:2 * k1], T.lland[k0:k1, r:r + 2, 0]).then_inc(S.lrow, 16)
-        V.wait_ge(S.lrow, 16)
-        V.tensor_scalar(T.lf[0:1, 2 * k0:2 * k1], T.lrow[0:1, 2 * k0:2 * k1], 0.0, 512.0, OP.max, OP.mult).then_inc(S.lf, 1)
-    if P.get("latepl"):
-        SY.wait_ge(S.qo, 1)
-        for q in range(8):
-            SY.dma_start(T.pl[16 * q:16 * q + 16, :], T.place[:, :]).then_inc(S.lpl, 16)
-            SY.dma_start(T.ofl[16 * q:16 * q + 16, :], T.of[:, :]).then_inc(S.lpl, 16)
 
-    waited = ["lb"] if sb else []
-    for items in P["rank"]:
-        if any(p[0][0] == "C" for p, _, _, _ in items) and "lb" not in waited:
+    waited = []
+    for n, items in enumerate(P["rank"]):
+        if n == P["selat"] and not sb:
+            sel_all()
+        if far and any(p[0][0] == "C" and p[2] >= chosen[P["lbat"]] for later in P["rank"][n:n + 1 + P["early"]] for p, _, _, _ in later) and "lb" not in waited:
             waited.append("lb")
             g.wait_ge(S.lf, 1)
             g.partition_broadcast(T.lb[:, 2 * k0:2 * k1], T.lf[0:1, 2 * k0:2 * k1], 128).then_inc(S.lb, 1)
-            g.wait_ge(S.sf, 1)
-            g.partition_broadcast(T.selb[:, 0:N], T.sf[0:1, 0:N], 128).then_inc(S.selb, 1)
+            if P["selat"] < 0:
+                sel_all()
         for p, _, _, _ in items:
             if p[0][0] == "E":
                 need = ["qw"]
             elif p[0][0] == "X":
-                need = ["qx%d" % i for i, (a, b) in enumerate(xp) if a <= p[2] and p[1] <= b]
+                need = ["qx%d" % i for i, (a, b) in enumerate(xp) if a < CAPP * p[2] and CAPP * (p[1] - 1) < b]
             else:
                 need = ["gq%d" % k for k in range(p[1], p[2] + 1)]
             for s in need:
@@ -279,57 +329,97 @@ def rank_program(g, core, T, topo):
                     waited.append(s)
                     g.wait_ge(S[s], 1)
         call(items, "src")
-    if "lb" not in waited:
-        g.wait_ge(S.sf, 1)
-        g.partition_broadcast(T.selb[:, 0:N], T.sf[0:1, 0:N], 128).then_inc(S.selb, 1)
 
-    if chosen:
-        if not sb:
+    both = sorted((r - k) % N for k in range(N) if k not in chosen and not (ownc and k == 0))
+    second = {h: N + i for i, h in enumerate(both)}
+    nres = N + len(both)
+    nt = 3 + len(both)
+    runs = []
+    for h in both:
+        if runs and runs[-1][1] == h:
+            runs[-1][1] = h + 1
+        else:
+            runs.append([h, h + 1])
+
+    def first_terms():
+        V.wait_ge(S.lpl, 32 * ng)
+        V.tensor_scalar(T.tm[0:pn, 0:16], T.ofl[0:pn, :], float(SLOTS), float(-CAPP * r), OP.mult, OP.add).then_inc(S.tm, 1)
+        V.tensor_copy(T.tm[0:pn, 16:32], T.pl[0:pn, :]).then_inc(S.tm, 1)
+        V.tensor_scalar(T.tm[0:pn, 32:48], T.pl[0:pn, :], float(CAPP * r), float(SLOTS), OP.is_lt, OP.mult).then_inc(S.tm, 1)
+        if nt < 8:
+            V.memset(T.tm[0:pn, 16 * nt:128], 0.0).then_inc(S.tm, 1)
+
+    def far_row():
+        V.wait_ge(S.lrow, 16)
+        V.tensor_scalar(T.lf[0:1, 2 * k0:2 * k1], T.lrow[0:1, 2 * k0:2 * k1], 0.0, 512.0, OP.max, OP.mult).then_inc(S.lf, 1)
+
+    noffy = [1]
+
+    def last_terms():
+        V.wait_ge(S.selb, 1)
+        for a, b in runs:
+            V.tensor_scalar(T.sel3[:, a:b], T.selb[:, a:b], (second[a] - a) * SLOTS / 512.0, None, OP.mult).then_inc(S.s3, 1)
+        V.wait_ge(S.s3, len(runs))
+        for i, h in enumerate(both):
+            V.tensor_scalar(T.tm[0:pn, 48 + 16 * i:64 + 16 * i], T.ofl[0:pn, :], float(h), T.sel3[0:pn, h:h + 1], OP.is_equal, OP.mult).then_inc(S.tm, 1)
+
+    def tree():
+        V.wait_ge(S.tm, nt + (nt < 8))
+        src = T.tm
+        for name, w in (("t4", 64), ("t2", 32), ("t1", 16)):
+            V.tensor_tensor(T[name][0:pn, :], src[0:pn, 0:w], src[0:pn, w:2 * w], OP.add).then_inc(S[name], 1)
+            V.wait_ge(S[name], 1)
+            src = T[name]
+        V.tensor_copy(T.offy[0:pn, :], T.t1[0:pn, :]).then_inc(S.offy, 1)
+        noffy[0] = spread(T.offy, S.offy, 1)
+
+    def own_expert():
+        if ownc:
+            V.wait_ge(S.og, 1)
+            V.quantize_mx(T.el[:, 256 * r:256 * r + 128], T.els[:, 256 * r:256 * r + 128], T.eo[:]).then_inc(S.qe, 1)
+
+    fillers = [first_terms, last_terms, own_expert, tree]
+    before, between = P["fillers"]
+    for f in fillers[:before]:
+        f()
+    if not sb:
+        far_row()
+        if P["selat"] < 0:
+            sel_row()
+        for f in fillers[before:between]:
+            f()
+
+    def offsets(i):
+        k = chosen[i]
+        if i < len(sb):
+            V.wait_ge(S["ls%d" % k], sb[i])
+        elif i == len(sb):
             V.wait_ge(S.lb, 1)
-        V.wait_ge(S.ib, 1)
-        vp = P["vpart"]
-        for i, k in enumerate(chosen):
-            if sb:
-                V.wait_ge(S["li%d" % k], sb)
-            V.tensor_scalar(T.offe[:, 32 * i:32 * i + 32], T.ib[:], T.lb[:, 2 * k:2 * k + 1], None, OP.add).then_inc(S["go%d" % k], 1)
-        for i, k in enumerate(chosen):
-            V.wait_ge(S["go%d" % k], 1)
-            V.tensor_copy(T.eg[:, 512 * i:512 * i + 16 * vp], T.ws[:].indirect(T.offe[:, 32 * i:32 * i + vp])).then_inc(S["gv%d" % k], 1)
-            C.wait_ge(S["go%d" % k], 1)
-            C.activation(T.eg[:, 512 * i + 16 * vp:512 * i + 512], T.ws[:].indirect(T.offe[:, 32 * i + vp:32 * i + 32]), COPY).then_inc(S["gs%d" % k], 1)
-            V.wait_ge(S["gv%d" % k], 1)
-            V.wait_ge(S["gs%d" % k], 1)
-            V.quantize_mx(T.cq[:, 128 * i:128 * i + 128], T.cqs[:, 128 * i:128 * i + 128], T.eg[:, 512 * i:512 * i + 512]).then_inc(S["gq%d" % k], 1)
+        col = T.lbs[:, k:k + 1] if i < len(sb) else T.lb[:, 2 * k:2 * k + 1]
+        V.tensor_scalar(T.offe[:, 32 * i:32 * i + 32], T.ib[:], col, None, OP.add).then_inc(S["go%d" % k], 1)
 
-    both = [(r - k) % N for k in range(N) if k not in chosen]
-    base, n = [], 0
-    for h in range(N):
-        base.append(n)
-        n += 2 if h in both else 1
-    nres = n
-    V.wait_ge(S.lpl, 256)
-    V.wait_ge(S.selb, 1)
-    V.tensor_scalar(T.sel3[:, 0:N], T.selb[:, 0:N], SLOTS / 512.0, None, OP.mult).then_inc(S.s3, 1)
-    V.wait_ge(S.s3, 1)
-    terms = [(T.ofl, float(SLOTS), None, OP.mult, None), (T.pl, float(-CAPP * r), None, OP.add, None), (T.pl, float(CAPP * r), float(SLOTS), OP.is_lt, OP.mult)]
-    if chosen:
-        terms += [(T.ofl, float(h), float(SLOTS), OP.is_gt, OP.mult) for h in both if h < N - 1]
-    else:
-        terms[0] = (T.ofl, float(2 * SLOTS), None, OP.mult, None)
-    terms += [(T.ofl, float(h), T.sel3[:, h:h + 1], OP.is_equal, OP.mult) for h in both]
-    for i, (src, s1, s2, o1, o2) in enumerate(terms):
-        out = T.tm[:, 16 * i:16 * i + 16]
-        (V.tensor_scalar(out, src[:], s1, s2, o1, o2) if o2 else V.tensor_scalar(out, src[:], s1, None, o1)).then_inc(S.tm, 1)
-    n = len(terms)
-    if n < 16:
-        V.memset(T.tm[:, 16 * n:256], 0.0).then_inc(S.tm, 1)
-    V.wait_ge(S.tm, n + (n < 16))
-    src = T.tm
-    for name, w in (("t8", 128), ("t4", 64), ("t2", 32), ("t1", 16)):
-        V.tensor_tensor(T[name][:], src[:, 0:w], src[:, w:2 * w], OP.add).then_inc(S[name], 1)
-        V.wait_ge(S[name], 1)
-        src = T[name]
-    V.tensor_copy(T.offy[:], T.t1[:]).then_inc(S.offy, 1)
+    offsets(0)
+    ahead = P["ahead"] and not (sb and far)
+    if ahead:
+        offsets(1)
+    for i, k in enumerate(chosen):
+        vp = P["vpart"] if i else P["vfirst"]
+        V.wait_ge(S["go%d" % k], 1)
+        V.tensor_copy(T.eg[:, 512 * i:512 * i + 16 * vp], T.ws[:].indirect(T.offe[:, 32 * i:32 * i + vp])).then_inc(S["gv%d" % k], 1)
+        late = sb and far and i + 1 == len(sb)
+        if sb and far and i == P["lfat"]:
+            far_row()
+        if i + 1 + ahead < len(chosen) and not late:
+            offsets(i + 1 + ahead)
+        C.wait_ge(S["go%d" % k], 1)
+        C.activation(T.eg[:, 512 * i + 16 * vp:512 * i + 512], T.ws[:].indirect(T.offe[:, 32 * i + vp:32 * i + 32]), COPY).then_inc(S["gs%d" % k], 1)
+        V.wait_ge(S["gv%d" % k], 1)
+        V.wait_ge(S["gs%d" % k], 1)
+        V.quantize_mx(T.cq[:, 128 * i:128 * i + 128], T.cqs[:, 128 * i:128 * i + 128], T.eg[:, 512 * i:512 * i + 512]).then_inc(S["gq%d" % k], 1)
+        if late:
+            offsets(i + 1)
+    for f in fillers[before if sb else between:]:
+        f()
 
     seen = []
     nv = ns = nm = 0
@@ -337,7 +427,7 @@ def rank_program(g, core, T, topo):
     for it in P["order"]:
         k, ja, jb = it[:3]
         h = (r - k) % N
-        need = [("qw", 1)] if k == 0 else [("e%d" % k, arrive(lambda p, to: p[0][0] != "X" and to == k))]
+        need = [("qe" if ownc else "qw", 1)] if k == 0 else [("e%d" % k, arrive(lambda p, to: p[0][0] != "X" and to == k))]
         for i, (a, b) in enumerate(P["mparts"]):
             if a <= jb and ja <= b:
                 if a == 0:
@@ -351,17 +441,18 @@ def rank_program(g, core, T, topo):
         c0, c1 = CAPP * ja, CAPP * (jb + 1)
         skip = PAD if c1 - c0 < 128 else 0
         for m in range(2 if h in both else 1):
-            e0 = 256 * h + 128 * m
+            eq, es, e0 = (T.wq, T.wqs, 128 * m) if k == 0 and not ownc else (T.el, T.els, 256 * h + 128 * m)
+            at = SLOTS * (second[h] if m else h)
             cuts = [(c0, c1)] if len(it) == 3 else [(c0, (c0 + c1) // 2), ((c0 + c1) // 2, c1)]
             for a, b in cuts:
                 bank = 512 * (nm % 8)
                 if nm >= 8:
                     TE.wait_ge(*who[nm - 8])
-                TE.matmul_mx(T.ps[:, bank:bank + skip + b - a], T.el[:, e0:e0 + 128], T.els[:, e0:e0 + 128],
+                TE.matmul_mx(T.ps[:, bank:bank + skip + b - a], eq[:, e0:e0 + 128], es[:, e0:e0 + 128],
                              T.xl[:, PAD + a - skip:PAD + b], T.xls[:, PAD + a - skip:PAD + b], True, True).then_inc(S.mm, 1)
                 nm += 1
-                out, src = T.res[:, SLOTS * (base[h] + m) + a:SLOTS * (base[h] + m) + b], T.ps[:, bank + skip:bank + skip + b - a]
-                if nm % 2:
+                out, src = T.res[:, at + a:at + b], T.ps[:, bank + skip:bank + skip + b - a]
+                if (nm + P["sfirst"]) % 2:
                     V.wait_ge(S.mm, nm)
                     V.tensor_copy(out, src).then_inc(S.evv, 1)
                     nv += 1
@@ -373,7 +464,7 @@ def rank_program(g, core, T, topo):
                     who.append((S.evs, ns))
 
     for q in (V, C):
-        q.wait_ge(S.offy, 1)
+        q.wait_ge(S.offy, noffy[0])
         q.wait_ge(S.evv, nv)
         q.wait_ge(S.evs, ns)
     V.tensor_copy(T.yb[:, 0:128], T.res[:, 0:SLOTS * nres].indirect(T.offy[:, 0:8])).then_inc(S.yv, 1)

from concourse.bass import DstId, RemoteDMATransfer
from concourse.mybir import dt, AluOpType, ActivationFunctionType

N, CAPP, TC = 8, 48, 256
SLOTS = N * CAPP
PAD = 128 - CAPP

LO, HI, L0, L1, ALL = (0, 8), (8, 8), (0, 4), (4, 4), (0, 16)
EC, ES, E0, E1 = ("Ec", 0, 1), ("Es", 0, 1), ("Ec", 0, 0), ("Ec", 1, 1)


def pair(what, a, b):
    return [((what, a, a), "D", a, L0), ((what, b, b), "D", b, L1)]


def one(what, k):
    return [((what, k, k), "D", k, LO)]


PLAN = {
    "chosen": (4, 5, 6, 7),
    "xparts": ((0, 192), (192, 384)),
    "xv": (2, 1),
    "mparts": ((0, 3), (4, 7)),
    "rank": [[(("Xs", 1, 2), "H", 6, LO), (("Xs", 3, 4), "H", 5, HI)], [(("Xc", 3, 3), "H", 1, LO), (("Xc", 4, 4), "H", 0, HI)],
             pair("Xc", 1, 2), [(EC, "H", 1, HI)], [(("Xs", 5, 7), "H", 6, HI)], pair("Xc", 5, 6), one("Xc", 7),
             [(EC, "D", 3, LO)], [(ES, "H", 5, HI), (ES, "D", 3, LO)],
             [(("Cc", 4, 4), "H", 0, HI)], [(("Cs", 4, 4), "H", 0, HI)]]
            + [one(w, k) for k in (5, 6, 7) for w in ("Cc", "Cs")],
    "help": {0: [one("Xc", 4), one("Cc", 4), one("Cs", 4)],
             1: [one("Xc", 3), [(EC, "D", 1, LO)], [(EC, "D", 2, LO)]],
             5: [one("Xs", 3), one("Xs", 4), [(ES, "D", 1, LO)], [(ES, "D", 2, LO)]],
             6: [one("Xs", k) for k in (1, 2, 5, 6, 7)]},
    "order": [(0, 4, 7), (3, 4, 7), (0, 0, 3), (3, 0, 3), (1, 0, 7), (5, 0, 7, "h"), (6, 0, 7, "h"), (2, 0, 7), (4, 0, 7, "h"), (7, 0, 7, "h")],
    "wfirst": False,
    "vpart": 12,
    "vfirst": 16,
    "ownc": True,
    "le": 2,
    "fill": True,
    "sy": 1,
    "early": 0,
    "selat": 0,
    "sb": (),
    "ahead": True,
    "groups": 2,
    "qwat": 1,
    "fillers": (2, 3),
    "sfirst": 1,
    "lfat": 0,
    "lbat": 0,
}

F8 = "float8_e4m3fn_x4"
NE = 2 * N
SCRATCH = {
    "ldr": ("dram", [128, 1], "int32"), "lland": ("dram", [N, 128, 1], "int32"),
    "snd": ("sbuf", [128, 24], "int32"), "off4": ("sbuf", [128, 24], "uint16"),
    "pl": ("sbuf", [128, 16], "int32"), "ofl": ("sbuf", [128, 16], "int32"),
    "selrow": ("sbuf", [1, 16], "int32"), "sf": ("sbuf", [1, 16], "float32"), "selb": ("sbuf", [128, 16], "float32"),
    "lrow": ("sbuf", [1, 16], "int32"), "lf": ("sbuf", [1, 16], "float32"), "lb": ("sbuf", [128, 16], "float32"),
    "lbs": ("sbuf", [128, N], "float32"),
    "ip": ("sbuf", [128, 32], "int32"), "iq": ("sbuf", [128, 32], "int32"), "ip15": ("sbuf", [128, 32], "int32"),
    "ib": ("sbuf", [128, 32], "int32"), "offe": ("sbuf", [128, 32 * N], "uint16"), "offo": ("sbuf", [128, 32], "uint16"),
    "sel3": ("sbuf", [128, 16], "float32"), "tm": ("sbuf", [128, 16 * 8], "float32"),
    "t4": ("sbuf", [128, 64], "float32"), "t2": ("sbuf", [128, 32], "float32"), "t1": ("sbuf", [128, 16], "float32"),
    "offy": ("sbuf", [128, 16], "uint16"),
    "xs": ("sbuf", [128, 4 * TC], "bfloat16"), "ws": ("sbuf", [128, 1024], "bfloat16"),
    "xt": ("sbuf", [128, 4 * SLOTS], "bfloat16"), "eg": ("sbuf", [128, 512 * N], "bfloat16"), "eo": ("sbuf", [128, 512], "bfloat16"),
    "xq": ("sbuf", [128, SLOTS], F8), "xqs": ("sbuf", [128, SLOTS], "uint8"),
    "wq": ("sbuf", [128, 256], F8), "wqs": ("sbuf", [128, 256], "uint8"),
    "cq": ("sbuf", [128, 128 * N], F8), "cqs": ("sbuf", [128, 128 * N], "uint8"),
    "xl": ("sbuf", [128, PAD + SLOTS], F8), "xls": ("sbuf", [128, PAD + SLOTS], "uint8"),
    "el": ("sbuf", [128, 128 * NE], F8), "els": ("sbuf", [128, 128 * NE], "uint8"),
    "ps": ("psum", [128, 4096], "float32"), "res": ("sbuf", [128, SLOTS * NE], "float32"), "yb": ("sbuf", [128, TC], "float32"),
    "hx": ("sbuf", [128, SLOTS], F8), "hxs": ("sbuf", [128, SLOTS], "uint8"),
    "he": ("sbuf", [128, 256], F8), "hes": ("sbuf", [128, 256], "uint8"),
    "hc": ("sbuf", [128, 128 * N], F8), "hcs": ("sbuf", [128, 128 * N], "uint8"),
}
SEMAPHORES = ["loc", "li", "ldr", "lsel", "lw", "lsnd", "lx", "lpl", "lrow", "y0", "iot", "ib0", "ib", "sf", "selb", "qw", "off4", "oo", "og", "qe",
              "qo", "lf", "lb", "s3", "yv", "ys", "offy", "mm", "evv", "evs", "tm", "t4", "t2", "t1"]
SEMAPHORES += ["e%d" % k for k in range(1, N)] + ["xin%d" % k for k in range(4)] + ["h%d" % k for k in range(8)]
SEMAPHORES += ["%s%d" % (a, k) for a in ("xgv", "xgs", "qx") for k in range(3)]
SEMAPHORES += ["%s%d" % (a, k) for a in ("go", "gv", "gs", "gq", "ls") for k in range(N)]


def bits(engs):
    m = 0
    for e in engs:
        m |= 1 << e
    return m


def helpers_of(c, topo):
    mine = [k for k in topo.cores_of(c) if k != c]
    return [k for k in mine if topo.die(k) != topo.die(c)] + [k for k in mine if topo.die(k) == topo.die(c)]


def u8(ap):
    return ap.bitcast(dt.uint8)


def rank_program(g, core, T, topo):
    S, P = T.sem, PLAN
    chosen = P["chosen"]
    rank = T.rank_of(core)
    own = [c for c in topo.cores_of(core) if T.rank_of(c) is not None]
    if not own:
        return
    r = T.rank_of(own[0])
    hlp = helpers_of(own[0], topo)
    dest = lambda k: T.cores[(r + k) % N]
    lo = topo.engines(core, dest(1))
    eng = lo + [e for e in topo.engines(core, [c for c in topo.cores_of(core) if c != core][0]) if e not in lo]
    sent = [0]

    def view(piece, where, k=None):
        what, a, b = piece
        sc = what[1] == "s"
        if what[0] == "X":
            name, c0, n = {"src": "xq", "mid": "hx", "dst": "xl"}[where], CAPP * (a - 1), CAPP * (b - a + 1)
            if where == "dst":
                c0 = PAD + CAPP * (N - k)
        elif what[0] == "E":
            name, c0, n = {"src": "wq", "mid": "he", "dst": "el"}[where], 128 * a, 128 * (b - a + 1)
            if where == "dst":
                c0 += 256 * r
        else:
            name, c0, n = {"src": "cq", "mid": "hc", "dst": "el"}[where], 128 * chosen.index(a), 128 * (b - a + 1)
            if where == "dst":
                c0 = 256 * r
        return T[name + "s"][:, c0:c0 + n] if sc else u8(T[name][:, c0:c0 + n])

    def xpart(k):
        return [i for i, (a, b) in enumerate(P["mparts"]) if a <= N - k <= b][0]

    def call(items, where):
        tr = []
        for piece, kind, to, (e0, n) in items:
            if kind == "D":
                c, dv = dest(to), view(piece, "dst", to)
                sem = S["xin%d" % xpart(to)] if piece[0][0] == "X" else S["e%d" % to]
            else:
                c, dv = hlp[to], view(piece, "mid")
                sem = S["h%d" % inbox(to).index(piece)]
            rid, pid = topo.addr(c, core)
            tr.append(RemoteDMATransfer(dst_ids=[DstId(rid=rid, pnc=pid)], dma_engine_mask=bits(eng[e0:e0 + n]), remote_sem=sem,
                                        srcs=[view(piece, where)], dsts=[dv]))
            sent[0] += n
        g.remote_dma_fused(tr, local_sem=S.loc)

    allcalls = list(P["rank"]) + [c for h in P["help"] for c in P["help"][h]]

    def inbox(h):
        return [p for items in allcalls for p, kind, to, e in items if kind == "H" and to == h]

    def inbox_n(h, piece):
        return [e[1] for items in allcalls for p, kind, to, e in items if kind == "H" and to == h and p == piece][0]

    def arrive(test):
        return sum(e[1] for items in allcalls for p, kind, to, e in items if kind == "D" and test(p, to))

    if rank is None:
        me = hlp.index(core)
        box, seen = inbox(me), []
        for items in P["help"].get(me, []):
            for p, kind, to, e in items:
                for i, q in enumerate(box):
                    if q[0] == p[0] and q[1] <= p[2] and p[1] <= q[2] and i not in seen:
                        seen.append(i)
                        g.wait_ge(S["h%d" % i], inbox_n(me, q))
            call(items, "mid")
        if sent[0]:
            g.wait_ge(S.loc, sent[0])
        return

    V, C, SY, TE = g.vector, g.scalar, g.sync, g.tensor
    COPY = ActivationFunctionType.Copy
    OP = AluOpType
    ownc = P["ownc"]

    sb = P["sb"]
    ng = P["groups"]
    pn = 16 * ng

    def spread(buf, sem, n):
        have = pn
        while have < 128:
            V.wait_ge(sem, n)
            V.tensor_copy(buf[have:2 * have, :], buf[0:have, :]).then_inc(sem, 1)
            have, n = 2 * have, n + 1
        return n

    far = chosen[len(sb):]
    if sb:
        SY.dma_start(T.selrow[0:1, :], T.sel[:, :]).then_inc(S.lsel, 16)
    if far:
        (C if sb else SY).dma_start(T.ldr[0:16, :], T.sel[:, :]).then_inc(S.ldr, 16)
        C.dma_start(T.ldr[16:128, :], T.place[0:7, :]).then_inc(S.ldr, 16)

    def load_w():
        (SY if ng < 8 else C).dma_start(T.ws[:, 0:512], T.w[0:128, :]).then_inc(S.lw, 16)
        SY.dma_start(T.ws[:, 512:1024], T.w[128:256, :]).then_inc(S.lw, 16)

    def load_send(qs, queue):
        for q in qs:
            queue.dma_start(T.snd[16 * q:16 * q + 16, :], T.send[:, :]).then_inc(S.lsnd, 16)

    if P["wfirst"]:
        load_w()
    load_send(range(P["sy"]), SY)
    SY.dma_start(T.xs[:], T.x[:]).then_inc(S.lx, 16)
    load_send(range(P["sy"], ng), C)
    if not sb:
        (C if ng < 8 else SY).dma_start(T.selrow[0:1, :], T.sel[:, :]).then_inc(S.lsel, 16)
    if not P["wfirst"]:
        load_w()
    for q in range(ng):
        SY.dma_start(T.pl[16 * q:16 * q + 16, :], T.place[:, :]).then_inc(S.lpl, 16)
        SY.dma_start(T.ofl[16 * q:16 * q + 16, :], T.of[:, :]).then_inc(S.lpl, 16)

    g.iota(T.ip[:], [[0, 32]], 0, 1).then_inc(S.iot, 1)
    g.iota(T.iq[:], [[16, 32]], 0, 0).then_inc(S.iot, 1)
    V.wait_ge(S.iot, 2)
    V.tensor_scalar(T.ip15[:], T.ip[:], 15, None, OP.bitwise_and).then_inc(S.ib0, 1)
    V.wait_ge(S.ib0, 1)
    V.tensor_tensor(T.ib[:], T.ip15[:], T.iq[:], OP.add).then_inc(S.ib, 1)

    def sel_row():
        V.wait_ge(S.lsel, 16)
        V.tensor_scalar(T.sf[0:1, :], T.selrow[0:1, :], 0.0, 512.0, OP.max, OP.mult).then_inc(S.sf, 1)

    def sel_all():
        g.wait_ge(S.sf, 1)
        g.partition_broadcast(T.selb[:, 0:N], T.sf[0:1, 0:N], 128).then_inc(S.selb, 1)

    tr, used = [], 0
    ident = lambda k: [DstId(rid=topo.addr(dest(N - k), core)[0], pnc=topo.addr(dest(N - k), core)[1])]
    if sb:
        sel_row()
        sel_all()
        g.wait_ge(S.selb, 1)
        for k, n in zip(chosen, sb):
            h = (r - k) % N
            tr.append(RemoteDMATransfer(dst_ids=ident(k), dma_engine_mask=bits(lo[used:used + n]), remote_sem=S["ls%d" % k],
                                        srcs=[T.selb[:, h:h + 1]], dsts=[T.lbs[:, k:k + 1]]))
            used += n
    nle = 0
    if far:
        g.wait_ge(S.ldr, 32)
        rest = lo[used:]
        two = min(len(far), len(rest) - len(far)) if P["le"] == 2 else 0
        le = [rest[2 * i:2 * i + 2] if i < two else rest[two + i:two + i + 1] for i in range(len(far))]
        nle = sum(len(e) for e in le)
        tr += [RemoteDMATransfer(dst_ids=ident(k), dma_engine_mask=bits(le[i]), remote_sem=S.li, srcs=[T.ldr[:, :]], dsts=[T.lland[k]])
               for i, k in enumerate(far)]
    g.remote_dma_fused(tr, local_sem=S.loc)
    sent[0] += nle + used

    def quant_w():
        V.wait_ge(S.lw, 32)
        V.quantize_mx(T.wq[:], T.wqs[:], T.ws[:]).then_inc(S.qw, 1)

    if P["wfirst"]:
        quant_w()
    V.wait_ge(S.lsnd, 16 * ng)
    a = 3 * ((r + 1) % N)
    V.tensor_scalar(T.off4[0:pn, 0:24 - a], T.snd[0:pn, a:24], 0.0, 4.0, OP.max, OP.mult).then_inc(S.off4, 1)
    if a:
        V.tensor_scalar(T.off4[0:pn, 24 - a:24], T.snd[0:pn, 0:a], 0.0, 4.0, OP.max, OP.mult).then_inc(S.off4, 1)
    noff = spread(T.off4, S.off4, 2 if a else 1)
    if not sb and P["selat"] >= 0:
        sel_row()
    for q in (V, C):
        q.wait_ge(S.off4, noff)
        q.wait_ge(S.lx, 16)
    xp = P["xparts"]
    for i in range(len(xp)):
        c0, c1, nv = xp[i][0], xp[i][1], P["xv"][i]
        for t in range(4):
            src = T.xs[:, t:4 * TC].indirect(T.off4[:, c0 // 16:c1 // 16])
            if t < nv:
                V.tensor_copy(T.xt[:, 4 * c0 + t:4 * c1:4], src).then_inc(S["xgv%d" % i], 1)
            else:
                C.activation(T.xt[:, 4 * c0 + t:4 * c1:4], src, COPY).then_inc(S["xgs%d" % i], 1)
        if i == P["qwat"] and not P["wfirst"]:
            quant_w()
        V.wait_ge(S["xgv%d" % i], nv)
        V.wait_ge(S["xgs%d" % i], 4 - nv)
        V.quantize_mx(T.xq[:, c0:c1], T.xqs[:, c0:c1], T.xt[:, 4 * c0:4 * c1]).then_inc(S["qx%d" % i], 1)

    V.wait_ge(S.ib, 1)
    if ownc:
        V.wait_ge(S.selb, 1)
        V.tensor_scalar(T.offo[:], T.ib[:], T.selb[:, r:r + 1], None, OP.add).then_inc(S.oo, 1)
        C.wait_ge(S.oo, 1)
        C.wait_ge(S.lw, 32)
        C.activation(T.eo[:], T.ws[:].indirect(T.offo[:]), COPY).then_inc(S.og, 1)

    def own_slots():
        V.quantize_mx(T.xl[:, 0:128], T.xls[:, 0:128], T.xt[:, 4 * (SLOTS - 128):4 * SLOTS]).then_inc(S.qo, 1)

    own_slots()

    if far:
        k0, k1 = min(far), max(far) + 1
        SY.wait_ge(S.li, nle)
        SY.dma_start(T.lrow[0:1, 2 * k0:2 * k1], T.lland[k0:k1, r:r + 2, 0]).then_inc(S.lrow, 16)

    waited = []
    for n, items in enumerate(P["rank"]):
        if n == P["selat"] and not sb:
            sel_all()
        if far and any(p[0][0] == "C" and p[2] >= chosen[P["lbat"]] for later in P["rank"][n:n + 1 + P["early"]] for p, _, _, _ in later) and "lb" not in waited:
            waited.append("lb")
            g.wait_ge(S.lf, 1)
            g.partition_broadcast(T.lb[:, 2 * k0:2 * k1], T.lf[0:1, 2 * k0:2 * k1], 128).then_inc(S.lb, 1)
            if P["selat"] < 0:
                sel_all()
        for p, _, _, _ in items:
            if p[0][0] == "E":
                need = ["qw"]
            elif p[0][0] == "X":
                need = ["qx%d" % i for i, (a, b) in enumerate(xp) if a < CAPP * p[2] and CAPP * (p[1] - 1) < b]
            else:
                need = ["gq%d" % k for k in range(p[1], p[2] + 1)]
            for s in need:
                if s not in waited:
                    waited.append(s)
                    g.wait_ge(S[s], 1)
        call(items, "src")

    both = sorted((r - k) % N for k in range(N) if k not in chosen and not (ownc and k == 0))
    second = {h: N + i for i, h in enumerate(both)}
    nres = N + len(both)
    nt = 3 + len(both)
    runs = []
    for h in both:
        if runs and runs[-1][1] == h:
            runs[-1][1] = h + 1
        else:
            runs.append([h, h + 1])

    def first_terms():
        V.wait_ge(S.lpl, 32 * ng)
        V.tensor_scalar(T.tm[0:pn, 0:16], T.ofl[0:pn, :], float(SLOTS), float(-CAPP * r), OP.mult, OP.add).then_inc(S.tm, 1)
        V.tensor_copy(T.tm[0:pn, 16:32], T.pl[0:pn, :]).then_inc(S.tm, 1)
        V.tensor_scalar(T.tm[0:pn, 32:48], T.pl[0:pn, :], float(CAPP * r), float(SLOTS), OP.is_lt, OP.mult).then_inc(S.tm, 1)
        if nt < 8:
            V.memset(T.tm[0:pn, 16 * nt:128], 0.0).then_inc(S.tm, 1)

    def far_row():
        V.wait_ge(S.lrow, 16)
        V.tensor_scalar(T.lf[0:1, 2 * k0:2 * k1], T.lrow[0:1, 2 * k0:2 * k1], 0.0, 512.0, OP.max, OP.mult).then_inc(S.lf, 1)

    noffy = [1]

    def last_terms():
        V.wait_ge(S.selb, 1)
        for a, b in runs:
            V.tensor_scalar(T.sel3[:, a:b], T.selb[:, a:b], (second[a] - a) * SLOTS / 512.0, None, OP.mult).then_inc(S.s3, 1)
        V.wait_ge(S.s3, len(runs))
        for i, h in enumerate(both):
            V.tensor_scalar(T.tm[0:pn, 48 + 16 * i:64 + 16 * i], T.ofl[0:pn, :], float(h), T.sel3[0:pn, h:h + 1], OP.is_equal, OP.mult).then_inc(S.tm, 1)

    def tree():
        V.wait_ge(S.tm, nt + (nt < 8))
        src = T.tm
        for name, w in (("t4", 64), ("t2", 32), ("t1", 16)):
            V.tensor_tensor(T[name][0:pn, :], src[0:pn, 0:w], src[0:pn, w:2 * w], OP.add).then_inc(S[name], 1)
            V.wait_ge(S[name], 1)
            src = T[name]
        V.tensor_copy(T.offy[0:pn, :], T.t1[0:pn, :]).then_inc(S.offy, 1)
        noffy[0] = spread(T.offy, S.offy, 1)

    def own_expert():
        if ownc:
            V.wait_ge(S.og, 1)
            V.quantize_mx(T.el[:, 256 * r:256 * r + 128], T.els[:, 256 * r:256 * r + 128], T.eo[:]).then_inc(S.qe, 1)

    fillers = [first_terms, last_terms, own_expert, tree]
    before, between = P["fillers"]
    for f in fillers[:before]:
        f()
    if not sb:
        far_row()
        if P["selat"] < 0:
            sel_row()
        for f in fillers[before:between]:
            f()

    def offsets(i):
        k = chosen[i]
        if i < len(sb):
            V.wait_ge(S["ls%d" % k], sb[i])
        elif i == len(sb):
            V.wait_ge(S.lb, 1)
        col = T.lbs[:, k:k + 1] if i < len(sb) else T.lb[:, 2 * k:2 * k + 1]
        V.tensor_scalar(T.offe[:, 32 * i:32 * i + 32], T.ib[:], col, None, OP.add).then_inc(S["go%d" % k], 1)

    offsets(0)
    ahead = P["ahead"] and not (sb and far)
    if ahead:
        offsets(1)
    for i, k in enumerate(chosen):
        vp = P["vpart"] if i else P["vfirst"]
        V.wait_ge(S["go%d" % k], 1)
        V.tensor_copy(T.eg[:, 512 * i:512 * i + 16 * vp], T.ws[:].indirect(T.offe[:, 32 * i:32 * i + vp])).then_inc(S["gv%d" % k], 1)
        late = sb and far and i + 1 == len(sb)
        if sb and far and i == P["lfat"]:
            far_row()
        if i + 1 + ahead < len(chosen) and not late:
            offsets(i + 1 + ahead)
        C.wait_ge(S["go%d" % k], 1)
        C.activation(T.eg[:, 512 * i + 16 * vp:512 * i + 512], T.ws[:].indirect(T.offe[:, 32 * i + vp:32 * i + 32]), COPY).then_inc(S["gs%d" % k], 1)
        V.wait_ge(S["gv%d" % k], 1)
        V.wait_ge(S["gs%d" % k], 1)
        V.quantize_mx(T.cq[:, 128 * i:128 * i + 128], T.cqs[:, 128 * i:128 * i + 128], T.eg[:, 512 * i:512 * i + 512]).then_inc(S["gq%d" % k], 1)
        if late:
            offsets(i + 1)
    for f in fillers[before if sb else between:]:
        f()

    seen = []
    nv = ns = nm = 0
    who = []
    for it in P["order"]:
        k, ja, jb = it[:3]
        h = (r - k) % N
        need = [("qe" if ownc else "qw", 1)] if k == 0 else [("e%d" % k, arrive(lambda p, to: p[0][0] != "X" and to == k))]
        for i, (a, b) in enumerate(P["mparts"]):
            if a <= jb and ja <= b:
                if a == 0:
                    need.append(("qo", 1))
                if b > 0:
                    need.append(("xin%d" % i, arrive(lambda p, to: p[0][0] == "X" and xpart(to) == i)))
        for s, cnt in need:
            if s not in seen:
                seen.append(s)
                TE.wait_ge(S[s], cnt)
        c0, c1 = CAPP * ja, CAPP * (jb + 1)
        skip = PAD if c1 - c0 < 128 else 0
        for m in range(2 if h in both else 1):
            eq, es, e0 = (T.wq, T.wqs, 128 * m) if k == 0 and not ownc else (T.el, T.els, 256 * h + 128 * m)
            at = SLOTS * (second[h] if m else h)
            cuts = [(c0, c1)] if len(it) == 3 else [(c0, (c0 + c1) // 2), ((c0 + c1) // 2, c1)]
            for a, b in cuts:
                bank = 512 * (nm % 8)
                if nm >= 8:
                    TE.wait_ge(*who[nm - 8])
                TE.matmul_mx(T.ps[:, bank:bank + skip + b - a], eq[:, e0:e0 + 128], es[:, e0:e0 + 128],
                             T.xl[:, PAD + a - skip:PAD + b], T.xls[:, PAD + a - skip:PAD + b], True, True).then_inc(S.mm, 1)
                nm += 1
                out, src = T.res[:, at + a:at + b], T.ps[:, bank + skip:bank + skip + b - a]
                if (nm + P["sfirst"]) % 2:
                    V.wait_ge(S.mm, nm)
                    V.tensor_copy(out, src).then_inc(S.evv, 1)
                    nv += 1
                    who.append((S.evv, nv))
                else:
                    C.wait_ge(S.mm, nm)
                    C.activation(out, src, COPY).then_inc(S.evs, 1)
                    ns += 1
                    who.append((S.evs, ns))

    for q in (V, C):
        q.wait_ge(S.offy, noffy[0])
        q.wait_ge(S.evv, nv)
        q.wait_ge(S.evs, ns)
    V.tensor_copy(T.yb[:, 0:128], T.res[:, 0:SLOTS * nres].indirect(T.offy[:, 0:8])).then_inc(S.yv, 1)
    C.activation(T.yb[:, 128:256], T.res[:, 0:SLOTS * nres].indirect(T.offy[:, 8:16]), COPY).then_inc(S.ys, 1)
    SY.wait_ge(S.yv, 1)
    SY.wait_ge(S.ys, 1)
    SY.dma_start(T.y[:, :], T.yb[:, :]).then_inc(S.y0, 16)
    SY.wait_ge(S.y0, 16)
    g.wait_ge(S.loc, sent[0])
